import numpy as np
import ml_dtypes


def mxq(x, axis, fmt="e4m3"):
    dtype, down = {"e4m3": (ml_dtypes.float8_e4m3fn, 7), "e5m2": (ml_dtypes.float8_e5m2, 14)}[fmt]
    v = np.moveaxis(np.asarray(x, np.float32).astype(ml_dtypes.bfloat16).astype(np.float64), axis, -1)
    blocks = v.reshape(v.shape[:-1] + (-1, 32))
    amax = np.abs(blocks).max(-1, keepdims=True)
    byte = np.maximum(np.where(amax > 0, np.frexp(amax)[1] - 1 + 127, 0) - down, 1)
    scale = np.exp2(byte - 127.0)
    codes = (blocks / scale).astype(np.float32).astype(dtype).astype(np.float64)
    return np.moveaxis((codes * scale).reshape(v.shape), -1, axis)


WIDE = False


def mx_kscale(k):
    if not WIDE:
        return np.ones(k)
    levels = np.array([10, -10, 5, -5, 0])
    if k % 512:
        return np.exp2(np.random.permutation(np.resize(levels, k // 32))).repeat(32)
    a = np.empty((k // 512, 16))
    for p in range(k // 512):
        a[p, :8] = np.random.permutation(np.resize(levels, 8))
        for g in range(8):
            far = levels[np.abs(levels - a[p, g]) >= 10]
            a[p, g + 8] = far[np.random.randint(len(far))]
    return np.exp2(a.ravel()).repeat(32)


BF16 = ml_dtypes.bfloat16


def bf(x):
    return np.asarray(x, np.float32).astype(BF16)


def f64(x):
    return np.asarray(x).astype(np.float64)


E2M1 = np.array([0.0, 0.5, 1.0, 1.5, 2.0, 3.0, 4.0, 6.0, -0.0, -0.5, -1.0, -1.5, -2.0, -3.0, -4.0, -6.0])


def pack_weight(w, fmt):
    k, n = w.shape
    w = f64(bf(w)).reshape(k // 32, 32, n)
    amax = np.abs(w).max(1)
    if fmt == "e4m3":
        byte = np.frexp(amax)[1] - 1 + 127 - 7
    else:
        mant, ex = np.frexp(amax / 6.0)
        byte = np.where(mant > 0.5, ex, ex - 1) + 127
    byte = np.clip(np.where(amax > 0, byte, 1), 1, 254)
    scaled = (w * np.exp2(127.0 - byte)[:, None, :]).reshape(k, n).astype(np.float32)
    by_word = np.ascontiguousarray(scaled.reshape(k // 512, 128, 4, n).transpose(0, 1, 3, 2))
    if fmt == "e4m3":
        words = by_word.astype(ml_dtypes.float8_e4m3fn).view(np.uint8)
    else:
        c = by_word.astype(ml_dtypes.float4_e2m1fn).view(np.uint8) & 0xF
        words = c[..., 0::2] | (c[..., 1::2] << 4)
    return np.ascontiguousarray(words), np.ascontiguousarray(byte.astype(np.uint8).reshape(k // 512, 16, n))


def unpack_weight(words, scales, fmt):
    g, p, n, _ = words.shape
    if fmt == "e4m3":
        vals = np.ascontiguousarray(words).view(ml_dtypes.float8_e4m3fn).astype(np.float64)
    else:
        nib = np.empty((g, p, n, 4), np.uint8)
        nib[..., 0::2] = words & 0xF
        nib[..., 1::2] = words >> 4
        vals = E2M1[nib]
    vals = vals * np.repeat(np.exp2(scales.astype(np.float64) - 127.0), 8, axis=1)[..., None]
    return vals.transpose(0, 1, 3, 2).reshape(g * 512, n)
def pack4(w):
    words, scales = pack_weight(w, "e2m1")
    return words.reshape(words.shape[0], 128, -1), scales


def unpack4(words, scales):
    return unpack_weight(words.reshape(words.shape[0], 128, -1, 2), scales, "e2m1")


L, D, G, Q = 1024, 512, 1536, 1024


def draw0():
    sd, sg = mx_kscale(D), mx_kscale(G)
    u = bf(np.random.standard_normal((L, D)) * sd[None, :])
    v_words, v_scales = pack4(np.random.standard_normal((D, G)) / np.sqrt(D) / sd[:, None])
    b = bf(np.random.standard_normal(G) * 0.5)
    t = bf(np.random.uniform(0.5, 1.5, L))
    p = bf(np.random.uniform(0.3, 1.0, G) * sg)
    a_words, a_scales = pack4(2.0 * np.random.standard_normal((G, Q)) / np.sqrt(G) / sg[:, None])
    c = bf(np.random.standard_normal(L) * 0.5)
    return {"u": u,
            "v_words": v_words,
            "v_scales": v_scales,
            "b": b,
            "t": t,
            "p": p,
            "a_words": a_words,
            "a_scales": a_scales,
            "c": c}


def growth_rate_change(u, v, b):
    s = mxq(u, 1, "e4m3") @ v
    return 0.4 * (s + b[None, :])


def core(u, v_words, v_scales, b, t, p, a_words, a_scales, c):
    rate = growth_rate_change(f64(u), unpack4(v_words, v_scales), f64(b))
    x = np.exp(f64(t)[:, None] * rate) - 1.0
    m = f64(p)[None, :] * x
    f = mxq(m, 1, "e4m3") @ unpack4(a_words, a_scales)
    return f + f64(c)[:, None]


def e4m3fn_bytes(y):
    return np.clip(np.asarray(y, np.float64), -448.0, 448.0).astype(np.float32).astype(ml_dtypes.float8_e4m3fn).view(np.uint8)


def e4m3fn_values(b):
    return np.asarray(b, np.uint8).view(ml_dtypes.float8_e4m3fn).astype(np.float64)


def setup_inputs():
    d = draw0()
    x0 = np.asarray(d['u']).astype(np.float64)
    s = (np.max(np.abs(x0), axis=(0,), keepdims=True) / 448.0).astype(np.float32)
    out = {}
    for k, v in d.items():
        if k == 'u':
            out['u_bytes'] = e4m3fn_bytes(x0 / s.astype(np.float64))
            out['u_scale'] = s
        else:
            out[k] = v
    return out


def reference(u_bytes, u_scale, v_words, v_scales, b, t, p, a_words, a_scales, c):
    return core(e4m3fn_values(u_bytes) * u_scale.astype(np.float64), v_words, v_scales, b, t, p, a_words, a_scales, c)

@@ -1,0 +1,357 @@
+from contextlib import ExitStack
+
+import concourse.mybir as mybir
+from concourse.masks import make_identity
+
+L, D, G, Q = 1024, 512, 1536, 1024
+FLOPS = 2 * L * D * G + 2 * L * G * Q
+
+F32 = mybir.dt.float32
+BF16 = mybir.dt.bfloat16
+I32 = mybir.dt.int32
+U32 = mybir.dt.uint32
+U16 = mybir.dt.uint16
+U8 = mybir.dt.uint8
+FP8 = mybir.dt.float8_e4m3fn
+FP8X4 = mybir.dt.float8_e4m3fn_x4
+FP4X4 = mybir.dt.float4_e2m1fn_x4
+ALU = mybir.AluOpType
+ACT = mybir.ActivationFunctionType
+
+P = 128
+PACK = 4
+K_PASS = P * PACK
+GROUPS = G // K_PASS
+TILES = L // P
+BANK = 512
+HALVES = Q // BANK
+CHUNKS = (2, 3, 2, 1)
+VECTOR_PLANES = 1
+RATE = 0.4
+
+
+def tile_knockoutpopulationgrowthguidereadout_w4_kernel(
+    tc, u_bytes, u_scale, v_words, v_scales, b, t, p, a_words, a_scales, c, out
+):
+    nc = tc.nc
+    first_tile = [sum(CHUNKS[:i]) for i in range(len(CHUNKS))]
+    units = [(ch, g) for ch in range(len(CHUNKS)) for g in range(GROUPS)]
+    last_chunk = len(CHUNKS) - 1
+    out_rows = out.rearrange("(p i) q -> p i q", i=TILES)
+    u_rows = u_bytes.rearrange("(p i) k -> p (i k)", i=TILES)
+
+    with ExitStack() as ctx:
+        keep = ctx.enter_context(tc.tile_pool(name="keep", bufs=1))
+        work = ctx.enter_context(tc.tile_pool(name="work", bufs=3))
+        psum = ctx.enter_context(tc.psum_pool(name="psum", bufs=1))
+        ctx.enter_context(tc.manual_schedule())
+
+        def kept(name, shape, dtype):
+            return keep.tile(shape, dtype, name=name, align_bytes=64)
+
+        def streamed(tag, index, shape, dtype, bufs):
+            return work.tile(shape, dtype, name="%s%d" % (tag, index), tag=tag, bufs=bufs, align_bytes=64)
+
+        def bank(tag, name, shape, dtype):
+            return psum.tile(shape, dtype, name=name, tag=tag, bufs={"scores": 4, "sums": 3, "turn": 1}[tag])
+
+        ident_bf = kept("ident_bf", [P, P], BF16)
+        ident_f32 = kept("ident_f32", [P, P], F32)
+        make_identity(nc, ident_bf[:])
+        make_identity(nc, ident_f32[:])
+
+        v_scale_raw = kept("v_scale_raw", [P, G], U8)
+        a_scale_sb = kept("a_scale_sb", [P, GROUPS, Q], U8)
+        nc.vector.memset(v_scale_raw[:].bitcast(I32), 0)
+        nc.vector.memset(a_scale_sb[:].bitcast(I32), 0)
+
+        u_raw = [kept("u_raw%d" % ch, [P, n * D], U8) for ch, n in enumerate(CHUNKS)]
+
+        def load_u(ch):
+            lo = first_tile[ch] * D
+            nc.sync.dma_start(out=u_raw[ch][:], in_=u_rows[:, lo : lo + CHUNKS[ch] * D])
+
+        u_scale_sb = kept("u_scale_sb", [P, PACK], F32)
+        t_col = kept("t_col", [P, TILES], BF16)
+        c_col = kept("c_col", [P, TILES], BF16)
+        b_col = kept("b_col", [P, GROUPS, PACK], BF16)
+        p_col = kept("p_col", [P, GROUPS, PACK], BF16)
+        v_word_raw = [kept("v_word_raw%d" % g, [P, 2 * K_PASS], U8) for g in range(GROUPS)]
+        a_word_sb = kept("a_word_sb", [P, GROUPS, 2 * Q], U8)
+
+        def load_v_words(g):
+            cols = slice(2 * g * K_PASS, 2 * (g + 1) * K_PASS)
+            nc.sync.dma_start(out=v_word_raw[g][:].bitcast(I32), in_=v_words[0][:, cols].bitcast(I32))
+
+        load_u(0)
+        nc.sync.dma_start(out=u_scale_sb[:], in_=u_scale.rearrange("o (p j) -> p (o j)", j=PACK))
+        nc.sync.dma_start(out=t_col[:], in_=t.rearrange("(p i) -> p i", i=TILES))
+        for r in range(4):
+            nc.sync.dma_start(out=v_scale_raw[r:P:32, :].bitcast(I32), in_=v_scales[0, r:16:4, :].bitcast(I32))
+        load_v_words(0)
+        nc.sync.dma_start(out=b_col[:], in_=b.rearrange("(g p j) -> p g j", p=P, j=PACK))
+        load_v_words(1)
+        load_v_words(2)
+        load_u(1)
+        nc.sync.dma_start(out=p_col[:], in_=p.rearrange("(g p j) -> p g j", p=P, j=PACK))
+        a_scale_rows = a_scales.rearrange("g (q r) n -> r q g n", r=4)
+        for r in range(4):
+            nc.sync.dma_start(out=a_scale_sb[r:P:32, :, :].bitcast(I32), in_=a_scale_rows[r].bitcast(I32))
+        nc.sync.dma_start(out=a_word_sb[:].bitcast(I32), in_=a_words.rearrange("g p n -> p g n").bitcast(I32))
+        nc.sync.dma_start(out=c_col[:], in_=c.rearrange("(p i) -> p i", i=TILES))
+        for ch in range(2, len(CHUNKS)):
+            load_u(ch)
+
+        u_wide = [kept("u_wide%d" % ch, [P, n * D], BF16) for ch, n in enumerate(CHUNKS)]
+        u_grouped = [kept("u_grouped%d" % ch, [P, n * P * PACK], BF16) for ch, n in enumerate(CHUNKS)]
+        u_codes = [kept("u_codes%d" % ch, [P, n * P], U32) for ch, n in enumerate(CHUNKS)]
+        u_plane = [kept("u_plane%d" % ch, [P, n * P], U8) for ch, n in enumerate(CHUNKS)]
+
+        def batches(ch):
+            return [range(lo, min(lo + 2, CHUNKS[ch])) for lo in range(0, CHUNKS[ch], 2)]
+
+        def widen_u(ch):
+            nc.scalar.copy(out=u_wide[ch][:], in_=u_raw[ch][:].bitcast(FP8))
+
+        def turn_u(ch, tiles):
+            turned = bank("turn", "turned%d_%d" % (ch, tiles[0]), [P, 2, len(tiles) * P], F32)
+            words = u_wide[ch][:].bitcast(F32)
+            for n, i in enumerate(tiles):
+                for w in range(2):
+                    nc.tensor.transpose(
+                        turned[:, w, n * P : (n + 1) * P], words[:, 256 * i + w : 256 * (i + 1) : 2], ident_f32[:]
+                    )
+            return turned
+
+        def scale_u(ch, tiles, turned):
+            width = len(tiles) * P
+            lo = tiles[0] * P * PACK
+            nc.vector.tensor_tensor(
+                out=u_grouped[ch][:, lo : lo + width * PACK].rearrange("p (n w e) -> p n w e", w=2, e=2),
+                in0=turned[:].bitcast(BF16).rearrange("p w (n e) -> p n w e", e=2),
+                in1=u_scale_sb[:].rearrange("p (w e) -> p w e", e=2).unsqueeze(1).broadcast_to([P, width, 2, 2]),
+                op=ALU.mult,
+            )
+
+        def quantise_u(ch):
+            nc.vector.quantize_mx(out=u_codes[ch][:].bitcast(FP8X4), scales=u_plane[ch][:], in_=u_grouped[ch][:])
+
+        v_word_sb = kept("v_word_sb", [P, 2 * G], U8)
+        v_scale_sb = kept("v_scale_sb", [P, G], U8)
+
+        def order_v_words(g):
+            cols = slice(g * K_PASS, (g + 1) * K_PASS)
+            nc.scalar.copy(
+                out=v_word_sb[:].bitcast(U16)[:, cols].rearrange("p (j m) -> p j m", j=PACK),
+                in_=v_word_raw[g][:].bitcast(U16).rearrange("p (m j) -> p j m", j=PACK),
+            )
+
+        def order_v_scales(g):
+            cols = slice(g * K_PASS, (g + 1) * K_PASS)
+            nc.vector.tensor_copy(
+                out=v_scale_sb[:, cols].rearrange("p (j m) -> p j m", j=PACK),
+                in_=v_scale_raw[:, cols].rearrange("p (m j) -> p j m", j=PACK),
+            )
+
+        scores, exponent, growth, planes, grouped = {}, {}, {}, {}, {}
+        m_codes = [kept("m_codes%d" % k, [P, CHUNKS[ch] * P], U32) for k, (ch, g) in enumerate(units)]
+        m_plane = [kept("m_plane%d" % k, [P, CHUNKS[ch] * P], U8) for k, (ch, g) in enumerate(units)]
+        t_spread = kept("t_spread", [P, L], BF16)
+        p_f32 = kept("p_f32", [P, GROUPS, PACK], F32)
+        p_neg = kept("p_neg", [P, GROUPS, PACK], F32)
+
+        def width_of(k):
+            return CHUNKS[units[k][0]] * P
+
+        def multiply_v(k):
+            ch, g = units[k]
+            width = width_of(k)
+            per_bank = BANK // width
+            pieces = [(lo, min(256, width - lo)) for lo in range(0, width, 256)] if width < BANK else [(0, BANK)]
+            for j in range(PACK):
+                if j % per_bank == 0:
+                    held = bank("scores", "scores%d_%d" % (k, j), [P, per_bank, width], F32)
+                scores[k, j] = held[:, j % per_bank, :]
+                col = (g * PACK + j) * P
+                for lo, n in pieces:
+                    nc.tensor.matmul_mx(
+                        out=held[:, j % per_bank, lo : lo + n],
+                        lhsT=v_word_sb[:, 2 * col : 2 * (col + P)].bitcast(FP4X4),
+                        lhsT_scale=v_scale_sb[:, col : col + P],
+                        rhs=u_codes[ch][:, lo : lo + n].bitcast(FP8X4),
+                        rhs_scale=u_plane[ch][:, lo : lo + n],
+                        start=True,
+                        stop=True,
+                    )
+
+        def bias_and_time(k, js):
+            ch, g = units[k]
+            width = width_of(k)
+            if k not in exponent:
+                exponent[k] = streamed("exponent", k, [P, PACK * width], F32, 3)
+            lo = first_tile[ch] * P
+            for j in js:
+                nc.vector.scalar_tensor_tensor(
+                    out=exponent[k][:, j * width : (j + 1) * width],
+                    in0=scores[k, j],
+                    scalar=b_col[:, g, j : j + 1],
+                    in1=t_spread[:, lo : lo + width],
+                    op0=ALU.add,
+                    op1=ALU.mult,
+                )
+
+        def exponentiate(k):
+            growth[k] = streamed("growth", k, [P, PACK * width_of(k)], F32, 3)
+            planes[k] = streamed("planes", k, [P, PACK * width_of(k)], BF16, 3)
+            nc.scalar.activation(out=growth[k][:], in_=exponent[k][:], func=ACT.Exp, scale=RATE)
+
+        def weigh_on_scalar(k):
+            g, width = units[k][1], width_of(k)
+            for j in range(VECTOR_PLANES, PACK):
+                cols = slice(j * width, (j + 1) * width)
+                nc.scalar.activation(
+                    out=planes[k][:, cols],
+                    in_=growth[k][:, cols],
+                    func=ACT.Identity,
+                    scale=p_f32[:, g, j : j + 1],
+                    bias=p_neg[:, g, j : j + 1],
+                )
+
+        def weigh_on_vector(k):
+            g, width = units[k][1], width_of(k)
+            for j in range(VECTOR_PLANES):
+                cols = slice(j * width, (j + 1) * width)
+                nc.vector.tensor_scalar(
+                    out=planes[k][:, cols],
+                    in0=growth[k][:, cols],
+                    scalar1=-1.0,
+                    scalar2=p_f32[:, g, j : j + 1],
+                    op0=ALU.add,
+                    op1=ALU.mult,
+                )
+
+        def interleave(k):
+            grouped[k] = streamed("grouped", k, [P, PACK * width_of(k)], BF16, 3)
+            nc.vector.tensor_copy(
+                out=grouped[k][:].rearrange("p (n i j) -> p n j i", i=4, j=PACK),
+                in_=planes[k][:].rearrange("p (j n i) -> p n j i", i=4, j=PACK),
+            )
+
+        def quantise_m(k):
+            nc.vector.quantize_mx(out=m_codes[k][:].bitcast(FP8X4), scales=m_plane[k][:], in_=grouped[k][:])
+
+        def multiply_a(sums, ch, n, h, g):
+            k = ch * GROUPS + g
+            nc.tensor.matmul_mx(
+                out=sums[:],
+                lhsT=m_codes[k][:, n * P : (n + 1) * P].bitcast(FP8X4),
+                lhsT_scale=m_plane[k][:, n * P : (n + 1) * P],
+                rhs=a_word_sb[:, g, 2 * h * BANK : 2 * (h + 1) * BANK].bitcast(FP4X4),
+                rhs_scale=a_scale_sb[:, g, h * BANK : (h + 1) * BANK],
+                start=(g == 0),
+                stop=(g == GROUPS - 1),
+            )
+
+        def finish(sums, ch, n, h, on_vector):
+            i = first_tile[ch] + n
+            result = streamed("result", i * HALVES + h, [P, BANK], F32, 8)
+            if on_vector:
+                nc.vector.tensor_scalar(
+                    out=result[:], in0=sums[:], scalar1=c_col[:, i : i + 1], scalar2=None, op0=ALU.add
+                )
+            else:
+                nc.scalar.activation(out=result[:], in_=sums[:], func=ACT.Identity, bias=c_col[:, i : i + 1])
+            nc.sync.dma_start(out=out_rows[:, i, h * BANK : (h + 1) * BANK], in_=result[:])
+
+        def readout(ch, n, h, on_vector):
+            sums = bank("sums", "sums%d_%d_%d" % (ch, n, h), [P, BANK], F32)
+            for g in range(GROUPS):
+                multiply_a(sums, ch, n, h, g)
+            finish(sums, ch, n, h, on_vector)
+
+        spread = bank("sums", "spread", [P, L], BF16)
+        for i in range(TILES):
+            nc.tensor.matmul(
+                spread[:, i * P : (i + 1) * P],
+                lhsT=t_col[:, i : i + 1].to_broadcast([P, P]),
+                rhs=ident_bf[:],
+                start=True,
+                stop=True,
+            )
+        widen_u(0)
+        order_v_words(0)
+        nc.scalar.copy(out=t_spread[:], in_=spread[:])
+        order_v_words(1)
+        order_v_scales(0)
+        for tiles in batches(0):
+            scale_u(0, tiles, turn_u(0, tiles))
+        order_v_scales(1)
+        quantise_u(0)
+        order_v_scales(2)
+        nc.vector.tensor_copy(out=p_f32[:], in_=p_col[:])
+        nc.vector.tensor_scalar(out=p_neg[:], in0=p_col[:], scalar1=-1.0, scalar2=None, op0=ALU.mult)
+
+        last_sums = []
+        for k in range(-2, len(units)):
+            ahead = k + 2 < len(units)
+            to_widen = [ch for ch in range(1, len(CHUNKS)) if GROUPS * ch - 5 == k]
+            to_scale = [(ch, tiles) for ch in range(1, len(CHUNKS)) if GROUPS * ch - 4 == k for tiles in batches(ch)]
+            to_quantise = [ch for ch in range(1, len(CHUNKS)) if GROUPS * ch - 3 == k]
+            done = k // GROUPS - 1
+            due = []
+            if done >= 0:
+                items = [(done, n, h) for n in range(CHUNKS[done]) for h in range(HALVES)]
+                share = -(-len(items) // GROUPS)
+                due = items[(k % GROUPS) * share : (k % GROUPS + 1) * share]
+
+            if ahead:
+                multiply_v(k + 2)
+            if 0 <= k + 1 < len(units):
+                exponentiate(k + 1)
+            for ch in to_widen:
+                widen_u(ch)
+            if k == -2:
+                order_v_words(2)
+            turned = turn_u(*to_scale[0]) if to_scale else None
+            if ahead:
+                for item in due:
+                    readout(*item, False)
+            if 0 <= k + 1 < len(units):
+                weigh_on_scalar(k + 1)
+
+            if k >= 0:
+                weigh_on_vector(k)
+            for ch in to_quantise:
+                quantise_u(ch)
+            if ahead:
+                bias_and_time(k + 2, range(0, 2))
+            else:
+                for item in due[0::2]:
+                    readout(*item, True)
+            if k >= 0:
+                interleave(k)
+            if to_scale:
+                scale_u(*to_scale[0], turned)
+            if ahead:
+                bias_and_time(k + 2, range(2, PACK))
+            else:
+                for item in due[1::2]:
+                    readout(*item, False)
+            if k >= 0:
+                quantise_m(k)
+            for ch, tiles in to_scale[1:]:
+                scale_u(ch, tiles, turn_u(ch, tiles))
+
+            if k >= 0 and units[k][0] == last_chunk:
+                g = units[k][1]
+                if g == 0:
+                    last_sums = [
+                        (bank("scores", "last%d_%d" % (n, h), [P, BANK], F32), n, h)
+                        for n in range(CHUNKS[last_chunk])
+                        for h in range(HALVES)
+                    ]
+                for sums, n, h in last_sums:
+                    multiply_a(sums, last_chunk, n, h, g)
+
+        for sums, n, h in last_sums:
+            finish(sums, last_chunk, n, h, h == 0)

@@ -25,8 +25,19 @@ GROUPS = G // K_PASS
 TILES = L // P
 BANK = 512
 HALVES = Q // BANK
-CHUNKS = (2, 3, 2, 1)
-VECTOR_PLANES = 1
+CHUNKS = (2, 2, 2, 2)
+WEIGH = "VVVV"
+WEIGH_TAIL = "VVSS"
+TAIL_UNITS = 2
+EMPTY = "S"
+FINISH_FROM = 0
+LEAD = 2
+LAST_TILE = 0
+TURN_TAG = "turn"
+WEIGH_HEAD = "VVSS"
+HEAD_UNITS = 3
+WEIGH_TAIL_UNITS = 2
+BANKS = {"scores": 2, "sums": 4, "turn": 2}
 RATE = 0.4
 
 
@@ -53,7 +64,7 @@ def tile_knockoutpopulationgrowthguidereadout_w4_kernel(
             return work.tile(shape, dtype, name="%s%d" % (tag, index), tag=tag, bufs=bufs, align_bytes=64)
 
         def bank(tag, name, shape, dtype):
-            return psum.tile(shape, dtype, name=name, tag=tag, bufs={"scores": 4, "sums": 3, "turn": 1}[tag])
+            return psum.tile(shape, dtype, name=name, tag=tag, bufs=BANKS[tag])
 
         ident_bf = kept("ident_bf", [P, P], BF16)
         ident_f32 = kept("ident_f32", [P, P], F32)
@@ -83,8 +94,8 @@ def tile_knockoutpopulationgrowthguidereadout_w4_kernel(
             cols = slice(2 * g * K_PASS, 2 * (g + 1) * K_PASS)
             nc.sync.dma_start(out=v_word_raw[g][:].bitcast(I32), in_=v_words[0][:, cols].bitcast(I32))
 
-        load_u(0)
         nc.sync.dma_start(out=u_scale_sb[:], in_=u_scale.rearrange("o (p j) -> p (o j)", j=PACK))
+        load_u(0)
         nc.sync.dma_start(out=t_col[:], in_=t.rearrange("(p i) -> p i", i=TILES))
         for r in range(4):
             nc.sync.dma_start(out=v_scale_raw[r:P:32, :].bitcast(I32), in_=v_scales[0, r:16:4, :].bitcast(I32))
@@ -110,11 +121,19 @@ def tile_knockoutpopulationgrowthguidereadout_w4_kernel(
         def batches(ch):
             return [range(lo, min(lo + 2, CHUNKS[ch])) for lo in range(0, CHUNKS[ch], 2)]
 
-        def widen_u(ch):
-            nc.scalar.copy(out=u_wide[ch][:], in_=u_raw[ch][:].bitcast(FP8))
+        scale_spread = kept("scale_spread", [P, D], F32)
+
+        def widen_u(ch, tiles):
+            cols = slice(tiles[0] * D, (tiles[-1] + 1) * D)
+            nc.vector.tensor_tensor(
+                out=u_wide[ch][:, cols].rearrange("p (i k) -> p i k", k=D),
+                in0=u_raw[ch][:, cols].bitcast(FP8).rearrange("p (i k) -> p i k", k=D),
+                in1=scale_spread[:].unsqueeze(1).broadcast_to([P, len(tiles), D]),
+                op=ALU.mult,
+            )
 
         def turn_u(ch, tiles):
-            turned = bank("turn", "turned%d_%d" % (ch, tiles[0]), [P, 2, len(tiles) * P], F32)
+            turned = bank(TURN_TAG, "turned%d_%d" % (ch, tiles[0]), [P, 2, len(tiles) * P], F32)
             words = u_wide[ch][:].bitcast(F32)
             for n, i in enumerate(tiles):
                 for w in range(2):
@@ -123,14 +142,11 @@ def tile_knockoutpopulationgrowthguidereadout_w4_kernel(
                     )
             return turned
 
-        def scale_u(ch, tiles, turned):
-            width = len(tiles) * P
-            lo = tiles[0] * P * PACK
-            nc.vector.tensor_tensor(
-                out=u_grouped[ch][:, lo : lo + width * PACK].rearrange("p (n w e) -> p n w e", w=2, e=2),
-                in0=turned[:].bitcast(BF16).rearrange("p w (n e) -> p n w e", e=2),
-                in1=u_scale_sb[:].rearrange("p (w e) -> p w e", e=2).unsqueeze(1).broadcast_to([P, width, 2, 2]),
-                op=ALU.mult,
+        def group_u(ch, tiles, turned):
+            cols = slice(tiles[0] * D, (tiles[-1] + 1) * D)
+            nc.scalar.copy(
+                out=u_grouped[ch][:, cols].bitcast(F32).rearrange("p (n w) -> p n w", w=2),
+                in_=turned[:].rearrange("p w n -> p n w"),
             )
 
         def quantise_u(ch):
@@ -153,7 +169,7 @@ def tile_knockoutpopulationgrowthguidereadout_w4_kernel(
                 in_=v_scale_raw[:, cols].rearrange("p (m j) -> p j m", j=PACK),
             )
 
-        scores, exponent, growth, planes, grouped = {}, {}, {}, {}, {}
+        scores, score_bank, exponent, growth, planes, grouped = {}, {}, {}, {}, {}, {}
         m_codes = [kept("m_codes%d" % k, [P, CHUNKS[ch] * P], U32) for k, (ch, g) in enumerate(units)]
         m_plane = [kept("m_plane%d" % k, [P, CHUNKS[ch] * P], U8) for k, (ch, g) in enumerate(units)]
         t_spread = kept("t_spread", [P, L], BF16)
@@ -163,14 +179,15 @@ def tile_knockoutpopulationgrowthguidereadout_w4_kernel(
         def width_of(k):
             return CHUNKS[units[k][0]] * P
 
-        def multiply_v(k):
+        def multiply_v(k, js):
             ch, g = units[k]
             width = width_of(k)
             per_bank = BANK // width
             pieces = [(lo, min(256, width - lo)) for lo in range(0, width, 256)] if width < BANK else [(0, BANK)]
-            for j in range(PACK):
+            for j in js:
                 if j % per_bank == 0:
-                    held = bank("scores", "scores%d_%d" % (k, j), [P, per_bank, width], F32)
+                    score_bank[k] = bank("scores", "scores%d_%d" % (k, j), [P, per_bank, width], F32)
+                held = score_bank[k]
                 scores[k, j] = held[:, j % per_bank, :]
                 col = (g * PACK + j) * P
                 for lo, n in pieces:
@@ -202,40 +219,55 @@ def tile_knockoutpopulationgrowthguidereadout_w4_kernel(
 
         def exponentiate(k):
             growth[k] = streamed("growth", k, [P, PACK * width_of(k)], F32, 3)
-            planes[k] = streamed("planes", k, [P, PACK * width_of(k)], BF16, 3)
+            planes[k] = streamed("planes", k, [P, PACK * width_of(k)], BF16, 4)
             nc.scalar.activation(out=growth[k][:], in_=exponent[k][:], func=ACT.Exp, scale=RATE)
 
-        def weigh_on_scalar(k):
+        def weigh(k, engine):
             g, width = units[k][1], width_of(k)
-            for j in range(VECTOR_PLANES, PACK):
+            plan = WEIGH_HEAD if k < HEAD_UNITS else WEIGH if k < len(units) - WEIGH_TAIL_UNITS else WEIGH_TAIL
+            for j in range(PACK):
+                if plan[j] != engine:
+                    continue
                 cols = slice(j * width, (j + 1) * width)
-                nc.scalar.activation(
-                    out=planes[k][:, cols],
-                    in_=growth[k][:, cols],
-                    func=ACT.Identity,
-                    scale=p_f32[:, g, j : j + 1],
-                    bias=p_neg[:, g, j : j + 1],
-                )
+                if engine == "S":
+                    nc.scalar.activation(
+                        out=planes[k][:, cols],
+                        in_=growth[k][:, cols],
+                        func=ACT.Identity,
+                        scale=p_f32[:, g, j : j + 1],
+                        bias=p_neg[:, g, j : j + 1],
+                    )
+                else:
+                    (nc.vector if engine == "V" else nc.gpsimd).tensor_scalar(
+                        out=planes[k][:, cols],
+                        in0=growth[k][:, cols],
+                        scalar1=-1.0,
+                        scalar2=p_f32[:, g, j : j + 1],
+                        op0=ALU.add,
+                        op1=ALU.mult,
+                    )
 
-        def weigh_on_vector(k):
-            g, width = units[k][1], width_of(k)
-            for j in range(VECTOR_PLANES):
-                cols = slice(j * width, (j + 1) * width)
-                nc.vector.tensor_scalar(
-                    out=planes[k][:, cols],
-                    in0=growth[k][:, cols],
-                    scalar1=-1.0,
-                    scalar2=p_f32[:, g, j : j + 1],
-                    op0=ALU.add,
-                    op1=ALU.mult,
+        def interleave(k, tiles):
+            woven = bank("turn", "woven%d_%d" % (k, tiles[0]), [P, len(tiles) * P * PACK], BF16)
+            by_token = planes[k][:].rearrange("p (j n) -> p n j", j=PACK)
+            for n, i in enumerate(tiles):
+                nc.tensor.matmul(
+                    woven[:, n * BANK : (n + 1) * BANK].rearrange("p (n j) -> p n j", j=PACK),
+                    lhsT=ident_bf[:],
+                    rhs=by_token[:, i * P : (i + 1) * P, :],
+                    start=True,
+                    stop=True,
                 )
+            return woven
 
-        def interleave(k):
-            grouped[k] = streamed("grouped", k, [P, PACK * width_of(k)], BF16, 3)
-            nc.vector.tensor_copy(
-                out=grouped[k][:].rearrange("p (n i j) -> p n j i", i=4, j=PACK),
-                in_=planes[k][:].rearrange("p (j n i) -> p n j i", i=4, j=PACK),
-            )
+        def empty(k, tiles, woven):
+            if k not in grouped:
+                grouped[k] = streamed("grouped", k, [P, PACK * width_of(k)], BF16, 3)
+            cols = slice(tiles[0] * BANK, (tiles[-1] + 1) * BANK)
+            if EMPTY[(k + tiles[0] // 2) % len(EMPTY)] == "V":
+                nc.vector.tensor_copy(out=grouped[k][:, cols], in_=woven[:])
+            else:
+                nc.scalar.copy(out=grouped[k][:, cols], in_=woven[:])
 
         def quantise_m(k):
             nc.vector.quantize_mx(out=m_codes[k][:].bitcast(FP8X4), scales=m_plane[k][:], in_=grouped[k][:])
@@ -269,6 +301,19 @@ def tile_knockoutpopulationgrowthguidereadout_w4_kernel(
                 multiply_a(sums, ch, n, h, g)
             finish(sums, ch, n, h, on_vector)
 
+        def interleave_on_vector(k):
+            grouped[k] = streamed("grouped", k, [P, PACK * width_of(k)], BF16, 3)
+            nc.vector.tensor_copy(
+                out=grouped[k][:].rearrange("p (n i j) -> p n j i", i=4, j=PACK),
+                in_=planes[k][:].rearrange("p (j n i) -> p n j i", i=4, j=PACK),
+            )
+
+        scales_turned = bank("sums", "scales_turned", [P, PACK, P], F32)
+        for j in range(PACK):
+            nc.tensor.transpose(scales_turned[:, j, :], u_scale_sb[:, j : j + 1].to_broadcast([P, P]), ident_f32[:])
+        nc.scalar.copy(
+            out=scale_spread[:].rearrange("p (n j) -> p n j", j=PACK), in_=scales_turned[:].rearrange("p j n -> p n j")
+        )
         spread = bank("sums", "spread", [P, L], BF16)
         for i in range(TILES):
             nc.tensor.matmul(
@@ -278,80 +323,80 @@ def tile_knockoutpopulationgrowthguidereadout_w4_kernel(
                 start=True,
                 stop=True,
             )
-        widen_u(0)
-        order_v_words(0)
-        nc.scalar.copy(out=t_spread[:], in_=spread[:])
-        order_v_words(1)
         order_v_scales(0)
-        for tiles in batches(0):
-            scale_u(0, tiles, turn_u(0, tiles))
+        order_v_words(0)
+        for i in range(CHUNKS[0]):
+            widen_u(0, [i])
+            group_u(0, [i], turn_u(0, [i]))
         order_v_scales(1)
         quantise_u(0)
+        nc.scalar.copy(out=t_spread[:], in_=spread[:])
+        order_v_words(1)
         order_v_scales(2)
+        order_v_words(2)
         nc.vector.tensor_copy(out=p_f32[:], in_=p_col[:])
         nc.vector.tensor_scalar(out=p_neg[:], in0=p_col[:], scalar1=-1.0, scalar2=None, op0=ALU.mult)
 
-        last_sums = []
-        for k in range(-2, len(units)):
-            ahead = k + 2 < len(units)
-            to_widen = [ch for ch in range(1, len(CHUNKS)) if GROUPS * ch - 5 == k]
-            to_scale = [(ch, tiles) for ch in range(1, len(CHUNKS)) if GROUPS * ch - 4 == k for tiles in batches(ch)]
-            to_quantise = [ch for ch in range(1, len(CHUNKS)) if GROUPS * ch - 3 == k]
-            done = k // GROUPS - 1
-            due = []
-            if done >= 0:
-                items = [(done, n, h) for n in range(CHUNKS[done]) for h in range(HALVES)]
-                share = -(-len(items) // GROUPS)
-                due = items[(k % GROUPS) * share : (k % GROUPS + 1) * share]
+        woven, turned_u, sums = [], [], {}
+        count = len(units)
 
-            if ahead:
-                multiply_v(k + 2)
-            if 0 <= k + 1 < len(units):
-                exponentiate(k + 1)
-            for ch in to_widen:
-                widen_u(ch)
-            if k == -2:
-                order_v_words(2)
-            turned = turn_u(*to_scale[0]) if to_scale else None
-            if ahead:
-                for item in due:
-                    readout(*item, False)
-            if 0 <= k + 1 < len(units):
-                weigh_on_scalar(k + 1)
+        def passes_due(step):
+            return [
+                (k, n)
+                for k in range(count)
+                for n in range(CHUNKS[units[k][0]])
+                if min(k + 1 + n, count) == step
+            ]
 
-            if k >= 0:
-                weigh_on_vector(k)
+        def accumulate(k, n):
+            ch, g = units[k]
+            for h in range(HALVES):
+                if g == 0:
+                    sums[ch, n, h] = bank("scores" if (ch, n) == (last_chunk, LAST_TILE) else "sums", "sums%d_%d_%d" % (ch, n, h), [P, BANK], F32)
+                multiply_a(sums[ch, n, h], ch, n, h, g)
+
+        multiply_v(0, range(PACK))
+        for k in range(-LEAD, count + 1):
+            biased, grown, mixed = k + LEAD, k + LEAD - 1, k + 1
+            ahead = biased < count
+            to_widen = [(ch, tiles) for ch in range(1, len(CHUNKS)) if GROUPS * ch - 3 == biased for tiles in batches(ch)]
+            to_quantise = [ch for ch in range(1, len(CHUNKS)) if GROUPS * ch - 2 == biased]
+            on_tensor = 0 <= mixed < count - TAIL_UNITS
+            weaving = batches(units[mixed][0]) if on_tensor else []
+            due = passes_due(k)
+
+            if 0 <= grown < count:
+                exponentiate(grown)
+            for tiles, held in woven:
+                empty(k, tiles, held)
+            for item in turned_u:
+                group_u(*item)
+            if 0 <= grown < count:
+                weigh(grown, "S")
+                weigh(grown, "G")
+            for item in due:
+                accumulate(*item)
+            closed = [(units[u][0], n, h) for u, n in due if units[u][1] == GROUPS - 1 for h in range(HALVES)]
+            if ahead:
+                bias_and_time(biased, range(0, 2))
+            if biased + 1 < count:
+                multiply_v(biased + 1, range(0, 2))
+            if max(0, count - TAIL_UNITS) <= k < count:
+                interleave_on_vector(k)
+            if ahead:
+                bias_and_time(biased, range(2, PACK))
+            if biased + 1 < count:
+                multiply_v(biased + 1, range(2, PACK))
+            for ch, n, h in closed:
+                finish(sums[ch, n, h], ch, n, h, biased >= count + FINISH_FROM and h == 0)
+            if 0 <= grown < count:
+                weigh(grown, "V")
             for ch in to_quantise:
                 quantise_u(ch)
-            if ahead:
-                bias_and_time(k + 2, range(0, 2))
-            else:
-                for item in due[0::2]:
-                    readout(*item, True)
-            if k >= 0:
-                interleave(k)
-            if to_scale:
-                scale_u(*to_scale[0], turned)
-            if ahead:
-                bias_and_time(k + 2, range(2, PACK))
-            else:
-                for item in due[1::2]:
-                    readout(*item, False)
-            if k >= 0:
+            if 0 <= k < count:
                 quantise_m(k)
-            for ch, tiles in to_scale[1:]:
-                scale_u(ch, tiles, turn_u(ch, tiles))
-
-            if k >= 0 and units[k][0] == last_chunk:
-                g = units[k][1]
-                if g == 0:
-                    last_sums = [
-                        (bank("scores", "last%d_%d" % (n, h), [P, BANK], F32), n, h)
-                        for n in range(CHUNKS[last_chunk])
-                        for h in range(HALVES)
-                    ]
-                for sums, n, h in last_sums:
-                    multiply_a(sums, last_chunk, n, h, g)
-
-        for sums, n, h in last_sums:
-            finish(sums, last_chunk, n, h, h == 0)
+            woven = [(tiles, interleave(mixed, tiles)) for tiles in weaving]
+            turned_u = []
+            for ch, tiles in to_widen:
+                widen_u(ch, tiles)
+                turned_u.append((ch, tiles, turn_u(ch, tiles)))

@@ -10,7 +10,6 @@ F32 = mybir.dt.float32
 BF16 = mybir.dt.bfloat16
 I32 = mybir.dt.int32
 U32 = mybir.dt.uint32
-U16 = mybir.dt.uint16
 U8 = mybir.dt.uint8
 FP8 = mybir.dt.float8_e4m3fn
 FP8X4 = mybir.dt.float8_e4m3fn_x4
@@ -25,19 +24,9 @@ GROUPS = G // K_PASS
 TILES = L // P
 BANK = 512
 HALVES = Q // BANK
-CHUNKS = (2, 2, 2, 2)
-WEIGH = "VVVV"
-WEIGH_TAIL = "VVSS"
-TAIL_UNITS = 2
-EMPTY = "S"
-FINISH_FROM = 0
-LEAD = 2
-LAST_TILE = 0
-TURN_TAG = "turn"
-WEIGH_HEAD = "VVSS"
-HEAD_UNITS = 3
-WEIGH_TAIL_UNITS = 2
-BANKS = {"scores": 2, "sums": 4, "turn": 2}
+BANKS = {"scores": 3, "turn": 3, "sums": 2}
+U_BATCHES = ((0, 1), (2, 3), (4, 5), (6, 7))
+CLOSE_LAG = 2
 RATE = 0.4
 
 
@@ -45,9 +34,6 @@ def tile_knockoutpopulationgrowthguidereadout_w4_kernel(
     tc, u_bytes, u_scale, v_words, v_scales, b, t, p, a_words, a_scales, c, out
 ):
     nc = tc.nc
-    first_tile = [sum(CHUNKS[:i]) for i in range(len(CHUNKS))]
-    units = [(ch, g) for ch in range(len(CHUNKS)) for g in range(GROUPS)]
-    last_chunk = len(CHUNKS) - 1
     out_rows = out.rearrange("(p i) q -> p i q", i=TILES)
     u_rows = u_bytes.rearrange("(p i) k -> p (i k)", i=TILES)
 
@@ -66,337 +52,278 @@ def tile_knockoutpopulationgrowthguidereadout_w4_kernel(
         def bank(tag, name, shape, dtype):
             return psum.tile(shape, dtype, name=name, tag=tag, bufs=BANKS[tag])
 
-        ident_bf = kept("ident_bf", [P, P], BF16)
-        ident_f32 = kept("ident_f32", [P, P], F32)
-        make_identity(nc, ident_bf[:])
-        make_identity(nc, ident_f32[:])
+        ident = kept("ident", [P, P], F32)
+        make_identity(nc, ident[:])
 
-        v_scale_raw = kept("v_scale_raw", [P, G], U8)
+        v_scale_sb = kept("v_scale_sb", [P, G], U8)
         a_scale_sb = kept("a_scale_sb", [P, GROUPS, Q], U8)
-        nc.vector.memset(v_scale_raw[:].bitcast(I32), 0)
+        b_row = kept("b_row", [P, G], BF16)
+        p_row = kept("p_row", [P, G], BF16)
+        ones = kept("ones", [P, P], BF16)
+        nc.vector.memset(b_row[:].bitcast(I32), 0)
+        nc.vector.memset(v_scale_sb[:].bitcast(I32), 0)
+        nc.vector.memset(ones[:], 1.0)
+        nc.vector.memset(p_row[:].bitcast(I32), 0)
         nc.vector.memset(a_scale_sb[:].bitcast(I32), 0)
 
-        u_raw = [kept("u_raw%d" % ch, [P, n * D], U8) for ch, n in enumerate(CHUNKS)]
+        u_raw = [kept("u_raw%d" % n, [P, len(tiles) * D], U8) for n, tiles in enumerate(U_BATCHES)]
 
-        def load_u(ch):
-            lo = first_tile[ch] * D
-            nc.sync.dma_start(out=u_raw[ch][:], in_=u_rows[:, lo : lo + CHUNKS[ch] * D])
+        def load_u(n):
+            tiles = U_BATCHES[n]
+            nc.sync.dma_start(out=u_raw[n][:], in_=u_rows[:, tiles[0] * D : (tiles[-1] + 1) * D])
 
         u_scale_sb = kept("u_scale_sb", [P, PACK], F32)
         t_col = kept("t_col", [P, TILES], BF16)
         c_col = kept("c_col", [P, TILES], BF16)
-        b_col = kept("b_col", [P, GROUPS, PACK], BF16)
-        p_col = kept("p_col", [P, GROUPS, PACK], BF16)
-        v_word_raw = [kept("v_word_raw%d" % g, [P, 2 * K_PASS], U8) for g in range(GROUPS)]
-        a_word_sb = kept("a_word_sb", [P, GROUPS, 2 * Q], U8)
-
-        def load_v_words(g):
-            cols = slice(2 * g * K_PASS, 2 * (g + 1) * K_PASS)
-            nc.sync.dma_start(out=v_word_raw[g][:].bitcast(I32), in_=v_words[0][:, cols].bitcast(I32))
+        v_word_sb = kept("v_word_sb", [P, 2 * G], U8)
+        a_word_sb = [kept("a_word_sb%d" % g, [P, 2 * Q], U8) for g in range(GROUPS)]
 
         nc.sync.dma_start(out=u_scale_sb[:], in_=u_scale.rearrange("o (p j) -> p (o j)", j=PACK))
         load_u(0)
-        nc.sync.dma_start(out=t_col[:], in_=t.rearrange("(p i) -> p i", i=TILES))
+        nc.sync.dma_start(out=b_row[0:1, :], in_=b.rearrange("(o g) -> o g", o=1))
         for r in range(4):
-            nc.sync.dma_start(out=v_scale_raw[r:P:32, :].bitcast(I32), in_=v_scales[0, r:16:4, :].bitcast(I32))
-        load_v_words(0)
-        nc.sync.dma_start(out=b_col[:], in_=b.rearrange("(g p j) -> p g j", p=P, j=PACK))
-        load_v_words(1)
-        load_v_words(2)
+            nc.sync.dma_start(out=v_scale_sb[r:P:32, :].bitcast(I32), in_=v_scales[0, r:16:4, :].bitcast(I32))
+        nc.sync.dma_start(out=v_word_sb[:].bitcast(I32), in_=v_words[0].bitcast(I32))
+        nc.sync.dma_start(out=t_col[:], in_=t.rearrange("(p i) -> p i", i=TILES))
         load_u(1)
-        nc.sync.dma_start(out=p_col[:], in_=p.rearrange("(g p j) -> p g j", p=P, j=PACK))
+        nc.sync.dma_start(out=p_row[0:1, :], in_=p.rearrange("(o g) -> o g", o=1))
         a_scale_rows = a_scales.rearrange("g (q r) n -> r q g n", r=4)
         for r in range(4):
             nc.sync.dma_start(out=a_scale_sb[r:P:32, :, :].bitcast(I32), in_=a_scale_rows[r].bitcast(I32))
-        nc.sync.dma_start(out=a_word_sb[:].bitcast(I32), in_=a_words.rearrange("g p n -> p g n").bitcast(I32))
+        for g in range(GROUPS):
+            nc.sync.dma_start(out=a_word_sb[g][:].bitcast(I32), in_=a_words[g].bitcast(I32))
         nc.sync.dma_start(out=c_col[:], in_=c.rearrange("(p i) -> p i", i=TILES))
-        for ch in range(2, len(CHUNKS)):
-            load_u(ch)
+        for n in range(2, len(U_BATCHES)):
+            load_u(n)
 
-        u_wide = [kept("u_wide%d" % ch, [P, n * D], BF16) for ch, n in enumerate(CHUNKS)]
-        u_grouped = [kept("u_grouped%d" % ch, [P, n * P * PACK], BF16) for ch, n in enumerate(CHUNKS)]
-        u_codes = [kept("u_codes%d" % ch, [P, n * P], U32) for ch, n in enumerate(CHUNKS)]
-        u_plane = [kept("u_plane%d" % ch, [P, n * P], U8) for ch, n in enumerate(CHUNKS)]
-
-        def batches(ch):
-            return [range(lo, min(lo + 2, CHUNKS[ch])) for lo in range(0, CHUNKS[ch], 2)]
-
-        scale_spread = kept("scale_spread", [P, D], F32)
-
-        def widen_u(ch, tiles):
-            cols = slice(tiles[0] * D, (tiles[-1] + 1) * D)
-            nc.vector.tensor_tensor(
-                out=u_wide[ch][:, cols].rearrange("p (i k) -> p i k", k=D),
-                in0=u_raw[ch][:, cols].bitcast(FP8).rearrange("p (i k) -> p i k", k=D),
-                in1=scale_spread[:].unsqueeze(1).broadcast_to([P, len(tiles), D]),
-                op=ALU.mult,
-            )
-
-        def turn_u(ch, tiles):
-            turned = bank(TURN_TAG, "turned%d_%d" % (ch, tiles[0]), [P, 2, len(tiles) * P], F32)
-            words = u_wide[ch][:].bitcast(F32)
-            for n, i in enumerate(tiles):
+        def turn(name, sources):
+            turned = bank("turn", name, [P, len(sources), 2, P], F32)
+            for n, source in enumerate(sources):
+                words = source.bitcast(F32)
                 for w in range(2):
-                    nc.tensor.transpose(
-                        turned[:, w, n * P : (n + 1) * P], words[:, 256 * i + w : 256 * (i + 1) : 2], ident_f32[:]
-                    )
+                    nc.tensor.transpose(turned[:, n, w, :], words[:, w : 2 * P : 2], ident[:])
             return turned
 
-        def group_u(ch, tiles, turned):
-            cols = slice(tiles[0] * D, (tiles[-1] + 1) * D)
+        def regroup(target, turned):
             nc.scalar.copy(
-                out=u_grouped[ch][:, cols].bitcast(F32).rearrange("p (n w) -> p n w", w=2),
-                in_=turned[:].rearrange("p w n -> p n w"),
+                out=target.bitcast(F32).rearrange("p (s n w) -> p s n w", n=P, w=2),
+                in_=turned[:].rearrange("p s w n -> p s n w"),
             )
 
-        def quantise_u(ch):
-            nc.vector.quantize_mx(out=u_codes[ch][:].bitcast(FP8X4), scales=u_plane[ch][:], in_=u_grouped[ch][:])
+        scales_turned = bank("sums", "scales_turned", [P, D], F32)
+        u_wide = [kept("u_wide%d" % n, [P, len(tiles) * D], BF16) for n, tiles in enumerate(U_BATCHES)]
+        u_grouped = [kept("u_grouped%d" % n, [P, len(tiles) * D], BF16) for n, tiles in enumerate(U_BATCHES)]
+        u_codes = kept("u_codes", [P, L], U32)
+        u_plane = kept("u_plane", [P, L], U8)
 
-        v_word_sb = kept("v_word_sb", [P, 2 * G], U8)
-        v_scale_sb = kept("v_scale_sb", [P, G], U8)
-
-        def order_v_words(g):
-            cols = slice(g * K_PASS, (g + 1) * K_PASS)
-            nc.scalar.copy(
-                out=v_word_sb[:].bitcast(U16)[:, cols].rearrange("p (j m) -> p j m", j=PACK),
-                in_=v_word_raw[g][:].bitcast(U16).rearrange("p (m j) -> p j m", j=PACK),
-            )
-
-        def order_v_scales(g):
-            cols = slice(g * K_PASS, (g + 1) * K_PASS)
-            nc.vector.tensor_copy(
-                out=v_scale_sb[:, cols].rearrange("p (j m) -> p j m", j=PACK),
-                in_=v_scale_raw[:, cols].rearrange("p (m j) -> p j m", j=PACK),
-            )
-
-        scores, score_bank, exponent, growth, planes, grouped = {}, {}, {}, {}, {}, {}
-        m_codes = [kept("m_codes%d" % k, [P, CHUNKS[ch] * P], U32) for k, (ch, g) in enumerate(units)]
-        m_plane = [kept("m_plane%d" % k, [P, CHUNKS[ch] * P], U8) for k, (ch, g) in enumerate(units)]
-        t_spread = kept("t_spread", [P, L], BF16)
-        p_f32 = kept("p_f32", [P, GROUPS, PACK], F32)
-        p_neg = kept("p_neg", [P, GROUPS, PACK], F32)
-
-        def width_of(k):
-            return CHUNKS[units[k][0]] * P
-
-        def multiply_v(k, js):
-            ch, g = units[k]
-            width = width_of(k)
-            per_bank = BANK // width
-            pieces = [(lo, min(256, width - lo)) for lo in range(0, width, 256)] if width < BANK else [(0, BANK)]
-            for j in js:
-                if j % per_bank == 0:
-                    score_bank[k] = bank("scores", "scores%d_%d" % (k, j), [P, per_bank, width], F32)
-                held = score_bank[k]
-                scores[k, j] = held[:, j % per_bank, :]
-                col = (g * PACK + j) * P
-                for lo, n in pieces:
-                    nc.tensor.matmul_mx(
-                        out=held[:, j % per_bank, lo : lo + n],
-                        lhsT=v_word_sb[:, 2 * col : 2 * (col + P)].bitcast(FP4X4),
-                        lhsT_scale=v_scale_sb[:, col : col + P],
-                        rhs=u_codes[ch][:, lo : lo + n].bitcast(FP8X4),
-                        rhs_scale=u_plane[ch][:, lo : lo + n],
-                        start=True,
-                        stop=True,
-                    )
-
-        def bias_and_time(k, js):
-            ch, g = units[k]
-            width = width_of(k)
-            if k not in exponent:
-                exponent[k] = streamed("exponent", k, [P, PACK * width], F32, 3)
-            lo = first_tile[ch] * P
-            for j in js:
-                nc.vector.scalar_tensor_tensor(
-                    out=exponent[k][:, j * width : (j + 1) * width],
-                    in0=scores[k, j],
-                    scalar=b_col[:, g, j : j + 1],
-                    in1=t_spread[:, lo : lo + width],
-                    op0=ALU.add,
-                    op1=ALU.mult,
+        def widen_u(n, places):
+            for s in places:
+                cols = slice(s * D, (s + 1) * D)
+                nc.vector.tensor_tensor(
+                    out=u_wide[n][:, cols], in0=u_raw[n][:, cols].bitcast(FP8), in1=scales_turned[:], op=ALU.mult
                 )
 
-        def exponentiate(k):
-            growth[k] = streamed("growth", k, [P, PACK * width_of(k)], F32, 3)
-            planes[k] = streamed("planes", k, [P, PACK * width_of(k)], BF16, 4)
-            nc.scalar.activation(out=growth[k][:], in_=exponent[k][:], func=ACT.Exp, scale=RATE)
+        def turn_u(n, places):
+            turned = turn("u_turned%d_%d" % (n, places[0]), [u_wide[n][:, s * D : (s + 1) * D] for s in places])
+            regroup(u_grouped[n][:, places[0] * D : (places[-1] + 1) * D], turned)
 
-        def weigh(k, engine):
-            g, width = units[k][1], width_of(k)
-            plan = WEIGH_HEAD if k < HEAD_UNITS else WEIGH if k < len(units) - WEIGH_TAIL_UNITS else WEIGH_TAIL
-            for j in range(PACK):
-                if plan[j] != engine:
-                    continue
-                cols = slice(j * width, (j + 1) * width)
-                if engine == "S":
-                    nc.scalar.activation(
-                        out=planes[k][:, cols],
-                        in_=growth[k][:, cols],
-                        func=ACT.Identity,
-                        scale=p_f32[:, g, j : j + 1],
-                        bias=p_neg[:, g, j : j + 1],
-                    )
-                else:
-                    (nc.vector if engine == "V" else nc.gpsimd).tensor_scalar(
-                        out=planes[k][:, cols],
-                        in0=growth[k][:, cols],
-                        scalar1=-1.0,
-                        scalar2=p_f32[:, g, j : j + 1],
-                        op0=ALU.add,
-                        op1=ALU.mult,
-                    )
+        def quantise_u(n, places):
+            cols = slice(U_BATCHES[n][places[0]] * P, (U_BATCHES[n][places[-1]] + 1) * P)
+            nc.vector.quantize_mx(
+                out=u_codes[:, cols].bitcast(FP8X4),
+                scales=u_plane[:, cols],
+                in_=u_grouped[n][:, places[0] * D : (places[-1] + 1) * D],
+            )
 
-        def interleave(k, tiles):
-            woven = bank("turn", "woven%d_%d" % (k, tiles[0]), [P, len(tiles) * P * PACK], BF16)
-            by_token = planes[k][:].rearrange("p (j n) -> p n j", j=PACK)
-            for n, i in enumerate(tiles):
-                nc.tensor.matmul(
-                    woven[:, n * BANK : (n + 1) * BANK].rearrange("p (n j) -> p n j", j=PACK),
-                    lhsT=ident_bf[:],
-                    rhs=by_token[:, i * P : (i + 1) * P, :],
-                    start=True,
-                    stop=True,
-                )
-            return woven
+        b_spread = kept("b_spread", [P, G], BF16)
+        p_spread = kept("p_spread", [P, G], BF16)
+        t_rate = kept("t_rate", [P, TILES], F32)
+        scores, biased, growth, m_rows, m_grouped, m_codes, m_plane, sums = {}, {}, {}, {}, {}, {}, {}, {}
 
-        def empty(k, tiles, woven):
-            if k not in grouped:
-                grouped[k] = streamed("grouped", k, [P, PACK * width_of(k)], BF16, 3)
-            cols = slice(tiles[0] * BANK, (tiles[-1] + 1) * BANK)
-            if EMPTY[(k + tiles[0] // 2) % len(EMPTY)] == "V":
-                nc.vector.tensor_copy(out=grouped[k][:, cols], in_=woven[:])
-            else:
-                nc.scalar.copy(out=grouped[k][:, cols], in_=woven[:])
+        def genes(gs):
+            return slice(gs[0] * K_PASS, (gs[-1] + 1) * K_PASS)
 
-        def quantise_m(k):
-            nc.vector.quantize_mx(out=m_codes[k][:].bitcast(FP8X4), scales=m_plane[k][:], in_=grouped[k][:])
+        def spread(tag, row, gs):
+            held = bank(tag, "spread_%s%d" % (tag, gs[0]), [P, len(gs) * K_PASS], BF16)
+            for n, g in enumerate(gs):
+                nc.tensor.matmul(held[:, genes([n])], lhsT=ones[:], rhs=row[:, genes([g])], start=True, stop=True)
+            return held
 
-        def multiply_a(sums, ch, n, h, g):
-            k = ch * GROUPS + g
+        def multiply_v(i, g):
+            scores[i, g] = bank("scores", "scores%d_%d" % (i, g), [P, BANK], F32)
             nc.tensor.matmul_mx(
-                out=sums[:],
-                lhsT=m_codes[k][:, n * P : (n + 1) * P].bitcast(FP8X4),
-                lhsT_scale=m_plane[k][:, n * P : (n + 1) * P],
-                rhs=a_word_sb[:, g, 2 * h * BANK : 2 * (h + 1) * BANK].bitcast(FP4X4),
+                out=scores[i, g][:],
+                lhsT=u_codes[:, i * P : (i + 1) * P].bitcast(FP8X4),
+                lhsT_scale=u_plane[:, i * P : (i + 1) * P],
+                rhs=v_word_sb[:, 2 * g * K_PASS : 2 * (g + 1) * K_PASS].bitcast(FP4X4),
+                rhs_scale=v_scale_sb[:, genes([g])],
+                start=True,
+                stop=True,
+            )
+
+        def add_bias(i, g):
+            if g == 0:
+                biased[i] = streamed("biased", i, [P, G], F32, 3)
+            nc.vector.tensor_tensor(
+                out=biased[i][:, genes([g])], in0=scores[i, g][:], in1=b_spread[:, genes([g])], op=ALU.add
+            )
+
+        def exponentiate(i, g):
+            if g == 0:
+                growth[i] = streamed("growth", i, [P, G], F32, 3)
+            nc.scalar.activation(
+                out=growth[i][:, genes([g])], in_=biased[i][:, genes([g])], func=ACT.Exp, scale=t_rate[:, i : i + 1]
+            )
+
+        def weigh(i, gs):
+            if gs[0] == 0:
+                m_rows[i] = streamed("m_rows", i, [P, G], BF16, 3)
+                m_grouped[i] = streamed("m_grouped", i, [P, G], BF16, 3)
+            nc.vector.scalar_tensor_tensor(
+                out=m_rows[i][:, genes(gs)],
+                in0=growth[i][:, genes(gs)],
+                scalar=-1.0,
+                in1=p_spread[:, genes(gs)],
+                op0=ALU.add,
+                op1=ALU.mult,
+            )
+
+        def turn_m(i, gs):
+            return turn("m_turned%d_%d" % (i, gs[0]), [m_rows[i][:, genes([g])] for g in gs])
+
+        def quantise_m(i, gs):
+            if gs[0] == 0:
+                m_codes[i] = streamed("m_codes", i, [P, GROUPS * P], U32, 3)
+                m_plane[i] = streamed("m_plane", i, [P, GROUPS * P], U8, 3)
+            cols = slice(gs[0] * P, (gs[-1] + 1) * P)
+            nc.vector.quantize_mx(
+                out=m_codes[i][:, cols].bitcast(FP8X4), scales=m_plane[i][:, cols], in_=m_grouped[i][:, genes(gs)]
+            )
+
+        def multiply_a(i, h, g, tag):
+            if g == 0:
+                sums[i, h] = bank(tag, "sums%d_%d" % (i, h), [P, BANK], F32)
+            nc.tensor.matmul_mx(
+                out=sums[i, h][:],
+                lhsT=m_codes[i][:, g * P : (g + 1) * P].bitcast(FP8X4),
+                lhsT_scale=m_plane[i][:, g * P : (g + 1) * P],
+                rhs=a_word_sb[g][:, 2 * h * BANK : 2 * (h + 1) * BANK].bitcast(FP4X4),
                 rhs_scale=a_scale_sb[:, g, h * BANK : (h + 1) * BANK],
                 start=(g == 0),
                 stop=(g == GROUPS - 1),
             )
 
-        def finish(sums, ch, n, h, on_vector):
-            i = first_tile[ch] + n
-            result = streamed("result", i * HALVES + h, [P, BANK], F32, 8)
+        def finish(i, h, on_vector):
+            result = streamed("result", i * HALVES + h, [P, BANK], F32, 6)
             if on_vector:
                 nc.vector.tensor_scalar(
-                    out=result[:], in0=sums[:], scalar1=c_col[:, i : i + 1], scalar2=None, op0=ALU.add
+                    out=result[:], in0=sums[i, h][:], scalar1=c_col[:, i : i + 1], scalar2=None, op0=ALU.add
                 )
             else:
-                nc.scalar.activation(out=result[:], in_=sums[:], func=ACT.Identity, bias=c_col[:, i : i + 1])
+                nc.scalar.activation(out=result[:], in_=sums[i, h][:], func=ACT.Identity, bias=c_col[:, i : i + 1])
             nc.sync.dma_start(out=out_rows[:, i, h * BANK : (h + 1) * BANK], in_=result[:])
 
-        def readout(ch, n, h, on_vector):
-            sums = bank("sums", "sums%d_%d_%d" % (ch, n, h), [P, BANK], F32)
+        def readout(i, h):
             for g in range(GROUPS):
-                multiply_a(sums, ch, n, h, g)
-            finish(sums, ch, n, h, on_vector)
+                multiply_a(i, h, g, "sums")
+            finish(i, h, False)
 
-        def interleave_on_vector(k):
-            grouped[k] = streamed("grouped", k, [P, PACK * width_of(k)], BF16, 3)
-            nc.vector.tensor_copy(
-                out=grouped[k][:].rearrange("p (n i j) -> p n j i", i=4, j=PACK),
-                in_=planes[k][:].rearrange("p (j n i) -> p n j i", i=4, j=PACK),
-            )
-
-        scales_turned = bank("sums", "scales_turned", [P, PACK, P], F32)
         for j in range(PACK):
-            nc.tensor.transpose(scales_turned[:, j, :], u_scale_sb[:, j : j + 1].to_broadcast([P, P]), ident_f32[:])
-        nc.scalar.copy(
-            out=scale_spread[:].rearrange("p (n j) -> p n j", j=PACK), in_=scales_turned[:].rearrange("p j n -> p n j")
-        )
-        spread = bank("sums", "spread", [P, L], BF16)
-        for i in range(TILES):
-            nc.tensor.matmul(
-                spread[:, i * P : (i + 1) * P],
-                lhsT=t_col[:, i : i + 1].to_broadcast([P, P]),
-                rhs=ident_bf[:],
-                start=True,
-                stop=True,
+            nc.tensor.transpose(
+                scales_turned[:, j:D:PACK], u_scale_sb[:, j : j + 1].to_broadcast([P, P]), ident[:]
             )
-        order_v_scales(0)
-        order_v_words(0)
-        for i in range(CHUNKS[0]):
-            widen_u(0, [i])
-            group_u(0, [i], turn_u(0, [i]))
-        order_v_scales(1)
-        quantise_u(0)
-        nc.scalar.copy(out=t_spread[:], in_=spread[:])
-        order_v_words(1)
-        order_v_scales(2)
-        order_v_words(2)
-        nc.vector.tensor_copy(out=p_f32[:], in_=p_col[:])
-        nc.vector.tensor_scalar(out=p_neg[:], in0=p_col[:], scalar1=-1.0, scalar2=None, op0=ALU.mult)
+        b_first, b_rest = spread("scores", b_row, [0]), spread("sums", b_row, [1, 2])
+        nc.scalar.copy(out=b_spread[:, genes([0])], in_=b_first[:])
+        widen_u(0, [0])
+        turn_u(0, [0])
+        widen_u(0, [1])
+        quantise_u(0, [0])
+        turn_u(0, [1])
+        for g in range(GROUPS):
+            multiply_v(0, g)
+        nc.scalar.copy(out=b_spread[:, genes([1, 2])], in_=b_rest[:])
+        nc.scalar.activation(out=t_rate[:], in_=t_col[:], func=ACT.Copy, scale=RATE)
 
-        woven, turned_u, sums = [], [], {}
-        count = len(units)
+        everything = list(range(GROUPS))
+        last = TILES - 1
 
-        def passes_due(step):
-            return [
-                (k, n)
-                for k in range(count)
-                for n in range(CHUNKS[units[k][0]])
-                if min(k + 1 + n, count) == step
-            ]
+        def turn_and_regroup(i, gs):
+            regroup(m_grouped[i][:, genes(gs)], turn_m(i, gs))
 
-        def accumulate(k, n):
-            ch, g = units[k]
+        def accumulate(i, h):
+            for g in range(GROUPS):
+                multiply_a(i, h, g, "sums")
+
+        both = [0, 1]
+        coarse = TILES - 2
+        for i in range(-1, coarse):
+            ahead = i + 1
+            to_widen = [n for n in range(1, len(U_BATCHES)) if n - 2 == i]
+            to_quantise = [n for n in range(1, len(U_BATCHES)) if n - 1 == i]
+            add_bias(ahead, 0)
+            exponentiate(ahead, 0)
+            if i >= 2:
+                finish(i - 2, 0, False)
+                accumulate(i - 2, 1)
+                finish(i - 2, 1, False)
+            if i >= 0:
+                weigh(i, everything)
+            for n in to_quantise:
+                quantise_u(n, both)
+            if i < 0:
+                quantise_u(0, [1])
+                p_held = [spread("turn", p_row, everything[:2]), spread("turn", p_row, everything[2:])]
+            if i >= 0:
+                turned = [turn_m(i, everything[:2]), turn_m(i, everything[2:])]
+            multiply_v(ahead + 1, 0)
+            add_bias(ahead, 1)
+            exponentiate(ahead, 1)
+            multiply_v(ahead + 1, 1)
+            add_bias(ahead, 2)
+            exponentiate(ahead, 2)
+            if i >= 0:
+                regroup(m_grouped[i][:, genes(everything[:2])], turned[0])
+                regroup(m_grouped[i][:, genes(everything[2:])], turned[1])
+            else:
+                nc.scalar.copy(out=p_spread[:, genes(everything[:2])], in_=p_held[0][:])
+                nc.scalar.copy(out=p_spread[:, genes(everything[2:])], in_=p_held[1][:])
+            if i >= 1:
+                quantise_m(i - 1, everything)
+                accumulate(i - 1, 0)
+            multiply_v(ahead + 1, 2)
+            for n in to_widen:
+                widen_u(n, both)
+                turn_u(n, both)
+
+        def close(i, g, tag):
+            quantise_m(i, [g])
             for h in range(HALVES):
-                if g == 0:
-                    sums[ch, n, h] = bank("scores" if (ch, n) == (last_chunk, LAST_TILE) else "sums", "sums%d_%d_%d" % (ch, n, h), [P, BANK], F32)
-                multiply_a(sums[ch, n, h], ch, n, h, g)
+                multiply_a(i, h, g, tag)
 
-        multiply_v(0, range(PACK))
-        for k in range(-LEAD, count + 1):
-            biased, grown, mixed = k + LEAD, k + LEAD - 1, k + 1
-            ahead = biased < count
-            to_widen = [(ch, tiles) for ch in range(1, len(CHUNKS)) if GROUPS * ch - 3 == biased for tiles in batches(ch)]
-            to_quantise = [ch for ch in range(1, len(CHUNKS)) if GROUPS * ch - 2 == biased]
-            on_tensor = 0 <= mixed < count - TAIL_UNITS
-            weaving = batches(units[mixed][0]) if on_tensor else []
-            due = passes_due(k)
-
-            if 0 <= grown < count:
-                exponentiate(grown)
-            for tiles, held in woven:
-                empty(k, tiles, held)
-            for item in turned_u:
-                group_u(*item)
-            if 0 <= grown < count:
-                weigh(grown, "S")
-                weigh(grown, "G")
-            for item in due:
-                accumulate(*item)
-            closed = [(units[u][0], n, h) for u, n in due if units[u][1] == GROUPS - 1 for h in range(HALVES)]
-            if ahead:
-                bias_and_time(biased, range(0, 2))
-            if biased + 1 < count:
-                multiply_v(biased + 1, range(0, 2))
-            if max(0, count - TAIL_UNITS) <= k < count:
-                interleave_on_vector(k)
-            if ahead:
-                bias_and_time(biased, range(2, PACK))
-            if biased + 1 < count:
-                multiply_v(biased + 1, range(2, PACK))
-            for ch, n, h in closed:
-                finish(sums[ch, n, h], ch, n, h, biased >= count + FINISH_FROM and h == 0)
-            if 0 <= grown < count:
-                weigh(grown, "V")
-            for ch in to_quantise:
-                quantise_u(ch)
-            if 0 <= k < count:
-                quantise_m(k)
-            woven = [(tiles, interleave(mixed, tiles)) for tiles in weaving]
-            turned_u = []
-            for ch, tiles in to_widen:
-                widen_u(ch, tiles)
-                turned_u.append((ch, tiles, turn_u(ch, tiles)))
+        tail = [(i, g) for i in (coarse, last) for g in range(GROUPS)]
+        finish(coarse - 2, 0, False)
+        accumulate(coarse - 2, 1)
+        for n, (i, g) in enumerate(tail):
+            if n < GROUPS:
+                add_bias(last, n)
+                exponentiate(last, n)
+            weigh(i, [g])
+            if n == 0:
+                finish(coarse - 2, 1, False)
+            turn_and_regroup(i, [g])
+            if n == 0:
+                quantise_m(coarse - 1, everything)
+                accumulate(coarse - 1, 0)
+            if n == 1:
+                accumulate(coarse - 1, 1)
+                finish(coarse - 1, 0, False)
+            if n == 2:
+                finish(coarse - 1, 1, False)
+            if n >= CLOSE_LAG:
+                i0, g0 = tail[n - CLOSE_LAG]
+                close(i0, g0, "scores" if i0 == coarse else "sums")
+        for i0, g0 in tail[len(tail) - CLOSE_LAG :]:
+            close(i0, g0, "sums")
+        for i in (coarse, last):
+            for h in range(HALVES):
+                finish(i, h, h == 0)

@@ -26,7 +26,8 @@ BANK = 512
 HALVES = Q // BANK
 BANKS = {"scores": 3, "turn": 3, "sums": 2}
 U_BATCHES = ((0, 1), (2, 3), (4, 5), (6, 7))
-CLOSE_LAG = 2
+U_LOADS = ((0, 1, 2, 3), (4, 5, 6, 7))
+SCALAR_TILES = 2
 RATE = 0.4
 
 
@@ -52,28 +53,29 @@ def tile_knockoutpopulationgrowthguidereadout_w4_kernel(
         def bank(tag, name, shape, dtype):
             return psum.tile(shape, dtype, name=name, tag=tag, bufs=BANKS[tag])
 
+        b_row = kept("b_row", [P, G], BF16)
+        nc.gpsimd.memset(b_row[:].bitcast(I32), 0)
         ident = kept("ident", [P, P], F32)
         make_identity(nc, ident[:])
 
         v_scale_sb = kept("v_scale_sb", [P, G], U8)
         a_scale_sb = kept("a_scale_sb", [P, GROUPS, Q], U8)
-        b_row = kept("b_row", [P, G], BF16)
         p_row = kept("p_row", [P, G], BF16)
         ones = kept("ones", [P, P], BF16)
-        nc.vector.memset(b_row[:].bitcast(I32), 0)
         nc.vector.memset(v_scale_sb[:].bitcast(I32), 0)
         nc.vector.memset(ones[:], 1.0)
-        nc.vector.memset(p_row[:].bitcast(I32), 0)
-        nc.vector.memset(a_scale_sb[:].bitcast(I32), 0)
+        nc.gpsimd.memset(p_row[:].bitcast(I32), 0)
+        nc.gpsimd.memset(a_scale_sb[:].bitcast(I32), 0)
 
-        u_raw = [kept("u_raw%d" % n, [P, len(tiles) * D], U8) for n, tiles in enumerate(U_BATCHES)]
+        u_raw = [kept("u_raw%d" % n, [P, len(tiles) * D], U8) for n, tiles in enumerate(U_LOADS)]
 
         def load_u(n):
-            tiles = U_BATCHES[n]
+            tiles = U_LOADS[n]
             nc.sync.dma_start(out=u_raw[n][:], in_=u_rows[:, tiles[0] * D : (tiles[-1] + 1) * D])
 
         u_scale_sb = kept("u_scale_sb", [P, PACK], F32)
         t_col = kept("t_col", [P, TILES], BF16)
+        p_col = kept("p_col", [P, PACK], BF16)
         c_col = kept("c_col", [P, TILES], BF16)
         v_word_sb = kept("v_word_sb", [P, 2 * G], U8)
         a_word_sb = [kept("a_word_sb%d" % g, [P, 2 * Q], U8) for g in range(GROUPS)]
@@ -85,23 +87,20 @@ def tile_knockoutpopulationgrowthguidereadout_w4_kernel(
             nc.sync.dma_start(out=v_scale_sb[r:P:32, :].bitcast(I32), in_=v_scales[0, r:16:4, :].bitcast(I32))
         nc.sync.dma_start(out=v_word_sb[:].bitcast(I32), in_=v_words[0].bitcast(I32))
         nc.sync.dma_start(out=t_col[:], in_=t.rearrange("(p i) -> p i", i=TILES))
-        load_u(1)
         nc.sync.dma_start(out=p_row[0:1, :], in_=p.rearrange("(o g) -> o g", o=1))
+        nc.sync.dma_start(out=p_col[:], in_=p[G - K_PASS :].rearrange("(m j) -> m j", j=PACK))
+        load_u(1)
         a_scale_rows = a_scales.rearrange("g (q r) n -> r q g n", r=4)
         for r in range(4):
             nc.sync.dma_start(out=a_scale_sb[r:P:32, :, :].bitcast(I32), in_=a_scale_rows[r].bitcast(I32))
         for g in range(GROUPS):
             nc.sync.dma_start(out=a_word_sb[g][:].bitcast(I32), in_=a_words[g].bitcast(I32))
         nc.sync.dma_start(out=c_col[:], in_=c.rearrange("(p i) -> p i", i=TILES))
-        for n in range(2, len(U_BATCHES)):
-            load_u(n)
 
-        def turn(name, sources):
-            turned = bank("turn", name, [P, len(sources), 2, P], F32)
-            for n, source in enumerate(sources):
-                words = source.bitcast(F32)
-                for w in range(2):
-                    nc.tensor.transpose(turned[:, n, w, :], words[:, w : 2 * P : 2], ident[:])
+        def turn(name, halves):
+            turned = bank("turn", name, [P, len(halves) // 2, 2, P], F32)
+            for n, words in enumerate(halves):
+                nc.tensor.transpose(turned[:, n // 2, n % 2, :], words, ident[:])
             return turned
 
         def regroup(target, turned):
@@ -119,12 +118,15 @@ def tile_knockoutpopulationgrowthguidereadout_w4_kernel(
         def widen_u(n, places):
             for s in places:
                 cols = slice(s * D, (s + 1) * D)
-                nc.vector.tensor_tensor(
-                    out=u_wide[n][:, cols], in0=u_raw[n][:, cols].bitcast(FP8), in1=scales_turned[:], op=ALU.mult
-                )
+                load, place = divmod(U_BATCHES[n][s], len(U_LOADS[0]))
+                codes = u_raw[load][:, place * D : (place + 1) * D].bitcast(FP8)
+                nc.vector.tensor_tensor(out=u_wide[n][:, cols], in0=codes, in1=scales_turned[:], op=ALU.mult)
 
         def turn_u(n, places):
-            turned = turn("u_turned%d_%d" % (n, places[0]), [u_wide[n][:, s * D : (s + 1) * D] for s in places])
+            turned = turn(
+                "u_turned%d_%d" % (n, places[0]),
+                [u_wide[n][:, s * D : (s + 1) * D].bitcast(F32)[:, w : 2 * P : 2] for s in places for w in range(2)],
+            )
             regroup(u_grouped[n][:, places[0] * D : (places[-1] + 1) * D], turned)
 
         def quantise_u(n, places):
@@ -149,6 +151,12 @@ def tile_knockoutpopulationgrowthguidereadout_w4_kernel(
                 nc.tensor.matmul(held[:, genes([n])], lhsT=ones[:], rhs=row[:, genes([g])], start=True, stop=True)
             return held
 
+        def keep_spread(target, gs, held):
+            nc.scalar.copy(
+                out=target[:, genes(gs)].bitcast(F32).rearrange("p (g w m) -> p g w m", w=2, m=P),
+                in_=held[:].bitcast(F32).rearrange("p (g m w) -> p g w m", w=2, m=P),
+            )
+
         def multiply_v(i, g):
             scores[i, g] = bank("scores", "scores%d_%d" % (i, g), [P, BANK], F32)
             nc.tensor.matmul_mx(
@@ -165,7 +173,10 @@ def tile_knockoutpopulationgrowthguidereadout_w4_kernel(
             if g == 0:
                 biased[i] = streamed("biased", i, [P, G], F32, 3)
             nc.vector.tensor_tensor(
-                out=biased[i][:, genes([g])], in0=scores[i, g][:], in1=b_spread[:, genes([g])], op=ALU.add
+                out=biased[i][:, genes([g])].rearrange("p (w m e) -> p w m e", w=2, e=2),
+                in0=scores[i, g][:].rearrange("p (m w e) -> p w m e", w=2, e=2),
+                in1=b_spread[:, genes([g])].rearrange("p (w m e) -> p w m e", w=2, e=2),
+                op=ALU.add,
             )
 
         def exponentiate(i, g):
@@ -188,8 +199,31 @@ def tile_knockoutpopulationgrowthguidereadout_w4_kernel(
                 op1=ALU.mult,
             )
 
+        p_plus = kept("p_plus", [P, PACK], F32)
+        p_minus = kept("p_minus", [P, PACK], F32)
+
+        def weigh_on_scalar(i):
+            turned = bank("turn", "growth_turned%d" % i, [P, PACK, P], F32)
+            for j in range(PACK):
+                lo = G - K_PASS + (j // 2) * 2 * P + j % 2
+                nc.tensor.transpose(turned[:, j, :], growth[i][:, lo : lo + 2 * P - j % 2 : 2], ident[:])
+            planes = streamed("planes", i, [P, PACK, P], BF16, 2)
+            for j in range(PACK):
+                nc.scalar.activation(
+                    out=planes[:, j, :],
+                    in_=turned[:, j, :],
+                    func=ACT.Identity,
+                    scale=p_plus[:, j : j + 1],
+                    bias=p_minus[:, j : j + 1],
+                )
+            nc.scalar.copy(
+                out=m_grouped[i][:, G - K_PASS :].rearrange("p (n s j) -> p n j s", s=4, j=PACK),
+                in_=planes[:].rearrange("p j (n s) -> p n j s", s=4),
+            )
+
         def turn_m(i, gs):
-            return turn("m_turned%d_%d" % (i, gs[0]), [m_rows[i][:, genes([g])] for g in gs])
+            words = m_rows[i][:, genes(gs)].bitcast(F32)
+            return turn("m_turned%d_%d" % (i, gs[0]), [words[:, n * P : (n + 1) * P] for n in range(2 * len(gs))])
 
         def quantise_m(i, gs):
             if gs[0] == 0:
@@ -233,15 +267,16 @@ def tile_knockoutpopulationgrowthguidereadout_w4_kernel(
                 scales_turned[:, j:D:PACK], u_scale_sb[:, j : j + 1].to_broadcast([P, P]), ident[:]
             )
         b_first, b_rest = spread("scores", b_row, [0]), spread("sums", b_row, [1, 2])
-        nc.scalar.copy(out=b_spread[:, genes([0])], in_=b_first[:])
+        keep_spread(b_spread, [0], b_first)
         widen_u(0, [0])
         turn_u(0, [0])
         widen_u(0, [1])
         quantise_u(0, [0])
         turn_u(0, [1])
+        widen_u(1, [0])
         for g in range(GROUPS):
             multiply_v(0, g)
-        nc.scalar.copy(out=b_spread[:, genes([1, 2])], in_=b_rest[:])
+        keep_spread(b_spread, [1, 2], b_rest)
         nc.scalar.activation(out=t_rate[:], in_=t_col[:], func=ACT.Copy, scale=RATE)
 
         everything = list(range(GROUPS))
@@ -267,14 +302,17 @@ def tile_knockoutpopulationgrowthguidereadout_w4_kernel(
                 accumulate(i - 2, 1)
                 finish(i - 2, 1, False)
             if i >= 0:
-                weigh(i, everything)
+                weigh(i, everything[:2] if i < SCALAR_TILES else everything)
+            if 0 <= i < SCALAR_TILES:
+                weigh_on_scalar(i)
             for n in to_quantise:
                 quantise_u(n, both)
             if i < 0:
                 quantise_u(0, [1])
-                p_held = [spread("turn", p_row, everything[:2]), spread("turn", p_row, everything[2:])]
+                p_held = [spread("turn", p_row, everything[:2])]
             if i >= 0:
-                turned = [turn_m(i, everything[:2]), turn_m(i, everything[2:])]
+                spans = [everything[:2]] if i < SCALAR_TILES else [everything[:2], everything[2:]]
+                turned = [turn_m(i, gs) for gs in spans]
             multiply_v(ahead + 1, 0)
             add_bias(ahead, 1)
             exponentiate(ahead, 1)
@@ -282,48 +320,53 @@ def tile_knockoutpopulationgrowthguidereadout_w4_kernel(
             add_bias(ahead, 2)
             exponentiate(ahead, 2)
             if i >= 0:
-                regroup(m_grouped[i][:, genes(everything[:2])], turned[0])
-                regroup(m_grouped[i][:, genes(everything[2:])], turned[1])
+                for gs, held in zip(spans, turned):
+                    regroup(m_grouped[i][:, genes(gs)], held)
             else:
-                nc.scalar.copy(out=p_spread[:, genes(everything[:2])], in_=p_held[0][:])
-                nc.scalar.copy(out=p_spread[:, genes(everything[2:])], in_=p_held[1][:])
+                keep_spread(p_spread, everything[:2], p_held[0])
+                nc.scalar.activation(out=p_plus[:], in_=p_col[:], func=ACT.Copy)
+                nc.scalar.activation(out=p_minus[:], in_=p_col[:], func=ACT.Copy, scale=-1.0)
             if i >= 1:
                 quantise_m(i - 1, everything)
                 accumulate(i - 1, 0)
             multiply_v(ahead + 1, 2)
+            if i == SCALAR_TILES - 2:
+                keep_spread(p_spread, [2], spread("turn", p_row, [2]))
             for n in to_widen:
-                widen_u(n, both)
+                widen_u(n, both[1:] if n == 1 else both)
                 turn_u(n, both)
 
-        def close(i, g, tag):
-            quantise_m(i, [g])
-            for h in range(HALVES):
-                multiply_a(i, h, g, tag)
+        def close(i, gs):
+            quantise_m(i, gs)
+            for g in gs:
+                for h in range(HALVES):
+                    multiply_a(i, h, g, "turn" if (i, h) == (last, 1) else "scores")
 
-        tail = [(i, g) for i in (coarse, last) for g in range(GROUPS)]
         finish(coarse - 2, 0, False)
         accumulate(coarse - 2, 1)
-        for n, (i, g) in enumerate(tail):
-            if n < GROUPS:
-                add_bias(last, n)
-                exponentiate(last, n)
-            weigh(i, [g])
-            if n == 0:
+        for g in everything:
+            add_bias(last, g)
+            exponentiate(last, g)
+            weigh(coarse, [g])
+            if g == 0:
                 finish(coarse - 2, 1, False)
-            turn_and_regroup(i, [g])
-            if n == 0:
+                turn_and_regroup(coarse, [0])
                 quantise_m(coarse - 1, everything)
-                accumulate(coarse - 1, 0)
-            if n == 1:
-                accumulate(coarse - 1, 1)
+            if g < HALVES:
+                accumulate(coarse - 1, g)
+            if g == 1:
                 finish(coarse - 1, 0, False)
-            if n == 2:
-                finish(coarse - 1, 1, False)
-            if n >= CLOSE_LAG:
-                i0, g0 = tail[n - CLOSE_LAG]
-                close(i0, g0, "scores" if i0 == coarse else "sums")
-        for i0, g0 in tail[len(tail) - CLOSE_LAG :]:
-            close(i0, g0, "sums")
-        for i in (coarse, last):
-            for h in range(HALVES):
-                finish(i, h, h == 0)
+        turn_and_regroup(coarse, [1, 2])
+        close(coarse, [0])
+        weigh(last, [0, 1])
+        turn_and_regroup(last, [0, 1])
+        close(coarse, [1, 2])
+        finish(coarse - 1, 1, False)
+        weigh(last, [2])
+        turn_and_regroup(last, [2])
+        close(last, [0, 1])
+        finish(coarse, 1, True)
+        finish(coarse, 0, False)
+        close(last, [2])
+        for h in range(HALVES):
+            finish(last, h, h == 1)

from contextlib import ExitStack

import concourse.mybir as mybir
from concourse.masks import make_identity

L, D, G, Q = 1024, 512, 1536, 1024
FLOPS = 2 * L * D * G + 2 * L * G * Q

F32 = mybir.dt.float32
BF16 = mybir.dt.bfloat16
I32 = mybir.dt.int32
U32 = mybir.dt.uint32
U8 = mybir.dt.uint8
FP8 = mybir.dt.float8_e4m3fn
FP8X4 = mybir.dt.float8_e4m3fn_x4
FP4X4 = mybir.dt.float4_e2m1fn_x4
ALU = mybir.AluOpType
ACT = mybir.ActivationFunctionType

P = 128
PACK = 4
K_PASS = P * PACK
GROUPS = G // K_PASS
TILES = L // P
BANK = 512
HALVES = Q // BANK
BANKS = {"scores": 3, "turn": 3, "sums": 2}
U_BATCHES = ((0, 1), (2, 3), (4, 5), (6, 7))
U_LOADS = ((0, 1, 2, 3), (4, 5, 6, 7))
SCALAR_TILES = 2
RATE = 0.4


def tile_knockoutpopulationgrowthguidereadout_w4_kernel(
    tc, u_bytes, u_scale, v_words, v_scales, b, t, p, a_words, a_scales, c, out
):
    nc = tc.nc
    out_rows = out.rearrange("(p i) q -> p i q", i=TILES)
    u_rows = u_bytes.rearrange("(p i) k -> p (i k)", i=TILES)

    with ExitStack() as ctx:
        keep = ctx.enter_context(tc.tile_pool(name="keep", bufs=1))
        work = ctx.enter_context(tc.tile_pool(name="work", bufs=3))
        psum = ctx.enter_context(tc.psum_pool(name="psum", bufs=1))
        ctx.enter_context(tc.manual_schedule())

        def kept(name, shape, dtype):
            return keep.tile(shape, dtype, name=name, align_bytes=64)

        def streamed(tag, index, shape, dtype, bufs):
            return work.tile(shape, dtype, name="%s%d" % (tag, index), tag=tag, bufs=bufs, align_bytes=64)

        def bank(tag, name, shape, dtype):
            return psum.tile(shape, dtype, name=name, tag=tag, bufs=BANKS[tag])

        b_row = kept("b_row", [P, G], BF16)
        nc.gpsimd.memset(b_row[:].bitcast(I32), 0)
        ident = kept("ident", [P, P], F32)
        make_identity(nc, ident[:])

        v_scale_sb = kept("v_scale_sb", [P, G], U8)
        a_scale_sb = kept("a_scale_sb", [P, GROUPS, Q], U8)
        p_row = kept("p_row", [P, G], BF16)
        ones = kept("ones", [P, P], BF16)
        nc.vector.memset(v_scale_sb[:].bitcast(I32), 0)
        nc.vector.memset(ones[:], 1.0)
        nc.gpsimd.memset(p_row[:].bitcast(I32), 0)
        nc.gpsimd.memset(a_scale_sb[:].bitcast(I32), 0)

        u_raw = [kept("u_raw%d" % n, [P, len(tiles) * D], U8) for n, tiles in enumerate(U_LOADS)]

        def load_u(n):
            tiles = U_LOADS[n]
            nc.sync.dma_start(out=u_raw[n][:], in_=u_rows[:, tiles[0] * D : (tiles[-1] + 1) * D])

        u_scale_sb = kept("u_scale_sb", [P, PACK], F32)
        t_col = kept("t_col", [P, TILES], BF16)
        p_col = kept("p_col", [P, PACK], BF16)
        c_col = kept("c_col", [P, TILES], BF16)
        v_word_sb = kept("v_word_sb", [P, 2 * G], U8)
        a_word_sb = [kept("a_word_sb%d" % g, [P, 2 * Q], U8) for g in range(GROUPS)]

        nc.sync.dma_start(out=u_scale_sb[:], in_=u_scale.rearrange("o (p j) -> p (o j)", j=PACK))
        load_u(0)
        nc.sync.dma_start(out=b_row[0:1, :], in_=b.rearrange("(o g) -> o g", o=1))
        for r in range(4):
            nc.sync.dma_start(out=v_scale_sb[r:P:32, :].bitcast(I32), in_=v_scales[0, r:16:4, :].bitcast(I32))
        nc.sync.dma_start(out=v_word_sb[:].bitcast(I32), in_=v_words[0].bitcast(I32))
        nc.sync.dma_start(out=t_col[:], in_=t.rearrange("(p i) -> p i", i=TILES))
        nc.sync.dma_start(out=p_row[0:1, :], in_=p.rearrange("(o g) -> o g", o=1))
        nc.sync.dma_start(out=p_col[:], in_=p[G - K_PASS :].rearrange("(m j) -> m j", j=PACK))
        load_u(1)
        a_scale_rows = a_scales.rearrange("g (q r) n -> r q g n", r=4)
        for r in range(4):
            nc.sync.dma_start(out=a_scale_sb[r:P:32, :, :].bitcast(I32), in_=a_scale_rows[r].bitcast(I32))
        for g in range(GROUPS):
            nc.sync.dma_start(out=a_word_sb[g][:].bitcast(I32), in_=a_words[g].bitcast(I32))
        nc.sync.dma_start(out=c_col[:], in_=c.rearrange("(p i) -> p i", i=TILES))

        def turn(name, halves):
            turned = bank("turn", name, [P, len(halves) // 2, 2, P], F32)
            for n, words in enumerate(halves):
                nc.tensor.transpose(turned[:, n // 2, n % 2, :], words, ident[:])
            return turned

        def regroup(target, turned):
            nc.scalar.copy(
                out=target.bitcast(F32).rearrange("p (s n w) -> p s n w", n=P, w=2),
                in_=turned[:].rearrange("p s w n -> p s n w"),
            )

        scales_turned = bank("sums", "scales_turned", [P, D], F32)
        u_wide = [kept("u_wide%d" % n, [P, len(tiles) * D], BF16) for n, tiles in enumerate(U_BATCHES)]
        u_grouped = [kept("u_grouped%d" % n, [P, len(tiles) * D], BF16) for n, tiles in enumerate(U_BATCHES)]
        u_codes = kept("u_codes", [P, L], U32)
        u_plane = kept("u_plane", [P, L], U8)

        def widen_u(n, places):
            for s in places:
                cols = slice(s * D, (s + 1) * D)
                load, place = divmod(U_BATCHES[n][s], len(U_LOADS[0]))
                codes = u_raw[load][:, place * D : (place + 1) * D].bitcast(FP8)
                nc.vector.tensor_tensor(out=u_wide[n][:, cols], in0=codes, in1=scales_turned[:], op=ALU.mult)

        def turn_u(n, places):
            turned = turn(
                "u_turned%d_%d" % (n, places[0]),
                [u_wide[n][:, s * D : (s + 1) * D].bitcast(F32)[:, w : 2 * P : 2] for s in places for w in range(2)],
            )
            regroup(u_grouped[n][:, places[0] * D : (places[-1] + 1) * D], turned)

        def quantise_u(n, places):
            cols = slice(U_BATCHES[n][places[0]] * P, (U_BATCHES[n][places[-1]] + 1) * P)
            nc.vector.quantize_mx(
                out=u_codes[:, cols].bitcast(FP8X4),
                scales=u_plane[:, cols],
                in_=u_grouped[n][:, places[0] * D : (places[-1] + 1) * D],
            )

        b_spread = kept("b_spread", [P, G], BF16)
        p_spread = kept("p_spread", [P, G], BF16)
        t_rate = kept("t_rate", [P, TILES], F32)
        scores, biased, growth, m_rows, m_grouped, m_codes, m_plane, sums = {}, {}, {}, {}, {}, {}, {}, {}

        def genes(gs):
            return slice(gs[0] * K_PASS, (gs[-1] + 1) * K_PASS)

        def spread(tag, row, gs):
            held = bank(tag, "spread_%s%d" % (tag, gs[0]), [P, len(gs) * K_PASS], BF16)
            for n, g in enumerate(gs):
                nc.tensor.matmul(held[:, genes([n])], lhsT=ones[:], rhs=row[:, genes([g])], start=True, stop=True)
            return held

        def keep_spread(target, gs, held):
            nc.scalar.copy(
                out=target[:, genes(gs)].bitcast(F32).rearrange("p (g w m) -> p g w m", w=2, m=P),
                in_=held[:].bitcast(F32).rearrange("p (g m w) -> p g w m", w=2, m=P),
            )

        def multiply_v(i, g):
            scores[i, g] = bank("scores", "scores%d_%d" % (i, g), [P, BANK], F32)
            nc.tensor.matmul_mx(
                out=scores[i, g][:],
                lhsT=u_codes[:, i * P : (i + 1) * P].bitcast(FP8X4),
                lhsT_scale=u_plane[:, i * P : (i + 1) * P],
                rhs=v_word_sb[:, 2 * g * K_PASS : 2 * (g + 1) * K_PASS].bitcast(FP4X4),
                rhs_scale=v_scale_sb[:, genes([g])],
                start=True,
                stop=True,
            )

        def add_bias(i, g):
            if g == 0:
                biased[i] = streamed("biased", i, [P, G], F32, 3)
            nc.vector.tensor_tensor(
                out=biased[i][:, genes([g])].rearrange("p (w m e) -> p w m e", w=2, e=2),
                in0=scores[i, g][:].rearrange("p (m w e) -> p w m e", w=2, e=2),
                in1=b_spread[:, genes([g])].rearrange("p (w m e) -> p w m e", w=2, e=2),
                op=ALU.add,
            )

        def exponentiate(i, g):
            if g == 0:
                growth[i] = streamed("growth", i, [P, G], F32, 3)
            nc.scalar.activation(
                out=growth[i][:, genes([g])], in_=biased[i][:, genes([g])], func=ACT.Exp, scale=t_rate[:, i : i + 1]
            )

        def weigh(i, gs):
            if gs[0] == 0:
                m_rows[i] = streamed("m_rows", i, [P, G], BF16, 3)
                m_grouped[i] = streamed("m_grouped", i, [P, G], BF16, 3)
            nc.vector.scalar_tensor_tensor(
                out=m_rows[i][:, genes(gs)],
                in0=growth[i][:, genes(gs)],
                scalar=-1.0,
                in1=p_spread[:, genes(gs)],
                op0=ALU.add,
                op1=ALU.mult,
            )

        p_plus = kept("p_plus", [P, PACK], F32)
        p_minus = kept("p_minus", [P, PACK], F32)

        def weigh_on_scalar(i):
            turned = bank("turn", "growth_turned%d" % i, [P, PACK, P], F32)
            for j in range(PACK):
                lo = G - K_PASS + (j // 2) * 2 * P + j % 2
                nc.tensor.transpose(turned[:, j, :], growth[i][:, lo : lo + 2 * P - j % 2 : 2], ident[:])
            planes = streamed("planes", i, [P, PACK, P], BF16, 2)
            for j in range(PACK):
                nc.scalar.activation(
                    out=planes[:, j, :],
                    in_=turned[:, j, :],
                    func=ACT.Identity,
                    scale=p_plus[:, j : j + 1],
                    bias=p_minus[:, j : j + 1],
                )
            nc.scalar.copy(
                out=m_grouped[i][:, G - K_PASS :].rearrange("p (n s j) -> p n j s", s=4, j=PACK),
                in_=planes[:].rearrange("p j (n s) -> p n j s", s=4),
            )

        def turn_m(i, gs):
            words = m_rows[i][:, genes(gs)].bitcast(F32)
            return turn("m_turned%d_%d" % (i, gs[0]), [words[:, n * P : (n + 1) * P] for n in range(2 * len(gs))])

        def quantise_m(i, gs):
            if gs[0] == 0:
                m_codes[i] = streamed("m_codes", i, [P, GROUPS * P], U32, 3)
                m_plane[i] = streamed("m_plane", i, [P, GROUPS * P], U8, 3)
            cols = slice(gs[0] * P, (gs[-1] + 1) * P)
            nc.vector.quantize_mx(
                out=m_codes[i][:, cols].bitcast(FP8X4), scales=m_plane[i][:, cols], in_=m_grouped[i][:, genes(gs)]
            )

        def multiply_a(i, h, g, tag):
            if g == 0:
                sums[i, h] = bank(tag, "sums%d_%d" % (i, h), [P, BANK], F32)
            nc.tensor.matmul_mx(
                out=sums[i, h][:],
                lhsT=m_codes[i][:, g * P : (g + 1) * P].bitcast(FP8X4),
                lhsT_scale=m_plane[i][:, g * P : (g + 1) * P],
                rhs=a_word_sb[g][:, 2 * h * BANK : 2 * (h + 1) * BANK].bitcast(FP4X4),
                rhs_scale=a_scale_sb[:, g, h * BANK : (h + 1) * BANK],
                start=(g == 0),
                stop=(g == GROUPS - 1),
            )

        def finish(i, h, on_vector):
            result = streamed("result", i * HALVES + h, [P, BANK], F32, 6)
            if on_vector:
                nc.vector.tensor_scalar(
                    out=result[:], in0=sums[i, h][:], scalar1=c_col[:, i : i + 1], scalar2=None, op0=ALU.add
                )
            else:
                nc.scalar.activation(out=result[:], in_=sums[i, h][:], func=ACT.Identity, bias=c_col[:, i : i + 1])
            nc.sync.dma_start(out=out_rows[:, i, h * BANK : (h + 1) * BANK], in_=result[:])

        def readout(i, h):
            for g in range(GROUPS):
                multiply_a(i, h, g, "sums")
            finish(i, h, False)

        for j in range(PACK):
            nc.tensor.transpose(
                scales_turned[:, j:D:PACK], u_scale_sb[:, j : j + 1].to_broadcast([P, P]), ident[:]
            )
        b_first, b_rest = spread("scores", b_row, [0]), spread("sums", b_row, [1, 2])
        keep_spread(b_spread, [0], b_first)
        widen_u(0, [0])
        turn_u(0, [0])
        widen_u(0, [1])
        quantise_u(0, [0])
        turn_u(0, [1])
        widen_u(1, [0])
        for g in range(GROUPS):
            multiply_v(0, g)
        keep_spread(b_spread, [1, 2], b_rest)
        nc.scalar.activation(out=t_rate[:], in_=t_col[:], func=ACT.Copy, scale=RATE)

        everything = list(range(GROUPS))
        last = TILES - 1

        def turn_and_regroup(i, gs):
            regroup(m_grouped[i][:, genes(gs)], turn_m(i, gs))

        def accumulate(i, h):
            for g in range(GROUPS):
                multiply_a(i, h, g, "sums")

        both = [0, 1]
        coarse = TILES - 2
        for i in range(-1, coarse):
            ahead = i + 1
            to_widen = [n for n in range(1, len(U_BATCHES)) if n - 2 == i]
            to_quantise = [n for n in range(1, len(U_BATCHES)) if n - 1 == i]
            add_bias(ahead, 0)
            exponentiate(ahead, 0)
            if i >= 2:
                finish(i - 2, 0, False)
                accumulate(i - 2, 1)
                finish(i - 2, 1, False)
            if i >= 0:
                weigh(i, everything[:2] if i < SCALAR_TILES else everything)
            if 0 <= i < SCALAR_TILES:
                weigh_on_scalar(i)
            for n in to_quantise:
                quantise_u(n, both)
            if i < 0:
                quantise_u(0, [1])
                p_held = [spread("turn", p_row, everything[:2])]
            if i >= 0:
                spans = [everything[:2]] if i < SCALAR_TILES else [everything[:2], everything[2:]]
                turned = [turn_m(i, gs) for gs in spans]
            multiply_v(ahead + 1, 0)
            add_bias(ahead, 1)
            exponentiate(ahead, 1)
            multiply_v(ahead + 1, 1)
            add_bias(ahead, 2)
            exponentiate(ahead, 2)
            if i >= 0:
                for gs, held in zip(spans, turned):
                    regroup(m_grouped[i][:, genes(gs)], held)
            else:
                keep_spread(p_spread, everything[:2], p_held[0])
                nc.scalar.activation(out=p_plus[:], in_=p_col[:], func=ACT.Copy)
                nc.scalar.activation(out=p_minus[:], in_=p_col[:], func=ACT.Copy, scale=-1.0)
            if i >= 1:
                quantise_m(i - 1, everything)
                accumulate(i - 1, 0)
            multiply_v(ahead + 1, 2)
            if i == SCALAR_TILES - 2:
                keep_spread(p_spread, [2], spread("turn", p_row, [2]))
            for n in to_widen:
                widen_u(n, both[1:] if n == 1 else both)
                turn_u(n, both)

        def close(i, gs):
            quantise_m(i, gs)
            for g in gs:
                for h in range(HALVES):
                    multiply_a(i, h, g, "turn" if (i, h) == (last, 1) else "scores")

        finish(coarse - 2, 0, False)
        accumulate(coarse - 2, 1)
        for g in everything:
            add_bias(last, g)
            exponentiate(last, g)
            weigh(coarse, [g])
            if g == 0:
                finish(coarse - 2, 1, False)
                turn_and_regroup(coarse, [0])
                quantise_m(coarse - 1, everything)
            if g < HALVES:
                accumulate(coarse - 1, g)
            if g == 1:
                finish(coarse - 1, 0, False)
        turn_and_regroup(coarse, [1, 2])
        close(coarse, [0])
        weigh(last, [0, 1])
        turn_and_regroup(last, [0, 1])
        close(coarse, [1, 2])
        finish(coarse - 1, 1, False)
        weigh(last, [2])
        turn_and_regroup(last, [2])
        close(last, [0, 1])
        finish(coarse, 1, True)
        finish(coarse, 0, False)
        close(last, [2])
        for h in range(HALVES):
            finish(last, h, h == 1)
